import numpy as np
import ml_dtypes


def mxq(x, axis, fmt="e4m3"):
    dtype, down = {"e4m3": (ml_dtypes.float8_e4m3fn, 7), "e5m2": (ml_dtypes.float8_e5m2, 14)}[fmt]
    v = np.moveaxis(np.asarray(x, np.float32).astype(ml_dtypes.bfloat16).astype(np.float64), axis, -1)
    blocks = v.reshape(v.shape[:-1] + (-1, 32))
    amax = np.abs(blocks).max(-1, keepdims=True)
    byte = np.maximum(np.where(amax > 0, np.frexp(amax)[1] - 1 + 127, 0) - down, 1)
    scale = np.exp2(byte - 127.0)
    codes = (blocks / scale).astype(np.float32).astype(dtype).astype(np.float64)
    return np.moveaxis((codes * scale).reshape(v.shape), -1, axis)


WIDE = False


def mx_kscale(k):
    if not WIDE:
        return np.ones(k)
    levels = np.array([10, -10, 5, -5, 0])
    if k % 512:
        return np.exp2(np.random.permutation(np.resize(levels, k // 32))).repeat(32)
    a = np.empty((k // 512, 16))
    for p in range(k // 512):
        a[p, :8] = np.random.permutation(np.resize(levels, 8))
        for g in range(8):
            far = levels[np.abs(levels - a[p, g]) >= 10]
            a[p, g + 8] = far[np.random.randint(len(far))]
    return np.exp2(a.ravel()).repeat(32)


def f64(x):
    return np.asarray(x).astype(np.float64)


def striped(idx):
    return np.tile(idx.reshape(-1, 16).T, (8, 1)).astype(np.uint16)


def unstriped(offs):
    return offs[:16].T.reshape(-1).astype(np.int64)


E2M1 = np.array([0.0, 0.5, 1.0, 1.5, 2.0, 3.0, 4.0, 6.0, -0.0, -0.5, -1.0, -1.5, -2.0, -3.0, -4.0, -6.0])


def pack_weight(w, fmt):
    k, n = w.shape
    w = f64(np.asarray(w, np.float32).astype(ml_dtypes.bfloat16)).reshape(k // 32, 32, n)
    amax = np.abs(w).max(1)
    if fmt == "e4m3":
        byte = np.frexp(amax)[1] - 1 + 127 - 7
    else:
        mant, ex = np.frexp(amax / 6.0)
        byte = np.where(mant > 0.5, ex, ex - 1) + 127
    byte = np.clip(np.where(amax > 0, byte, 1), 1, 254)
    scaled = (w * np.exp2(127.0 - byte)[:, None, :]).reshape(k, n).astype(np.float32)
    by_word = np.ascontiguousarray(scaled.reshape(k // 512, 128, 4, n).transpose(0, 1, 3, 2))
    if fmt == "e4m3":
        words = by_word.astype(ml_dtypes.float8_e4m3fn).view(np.uint8)
    else:
        c = by_word.astype(ml_dtypes.float4_e2m1fn).view(np.uint8) & 0xF
        words = (c[..., 0::2] | (c[..., 1::2] << 4)).reshape(k // 512, 128, 2 * n)
    return np.ascontiguousarray(words), np.ascontiguousarray(byte.astype(np.uint8).reshape(k // 512, 16, n))


def unpack_weight(words, scales, fmt):
    g, _, n = scales.shape
    words = np.ascontiguousarray(words).reshape(g, 128, n, -1)
    if fmt == "e4m3":
        vals = words.view(ml_dtypes.float8_e4m3fn).astype(np.float64)
    else:
        nib = np.empty((g, 128, n, 4), np.uint8)
        nib[..., 0::2] = words & 0xF
        nib[..., 1::2] = words >> 4
        vals = E2M1[nib]
    vals = vals * np.repeat(np.exp2(scales.astype(np.float64) - 127.0), 8, axis=1)[..., None]
    return vals.transpose(0, 1, 3, 2).reshape(g * 512, n)


def gelu(v):
    return 0.5 * v * (1.0 + np.tanh(np.sqrt(2.0 / np.pi) * (v + 0.044715 * v**3)))


K, H, T, S, T2, S2 = 1536, 1024, 2048, 512, 2048, 1024

def setup_inputs():
    n = np.random.standard_normal
    s = mx_kscale(K)[:, None]
    u = mx_kscale(H)[:, None]
    tab_words, tab_scales = pack_weight(n((K, T)) * s, "e4m3")
    tab2_words, tab2_scales = pack_weight(1.5 * n((H, T2)) / np.sqrt(H) / u, "e4m3")
    w4_words, w4_scales = pack_weight(n((K, H)) / np.sqrt(K) / s * u.T, "e2m1")
    w1 = (n((K, H)) / np.sqrt(K) / s).astype(np.float32)
    offs = striped(np.random.permutation(T)[:S])
    offs2 = striped(np.random.permutation(T2)[:S2])
    return {"tab_words": tab_words, "tab_scales": tab_scales,
            "tab2_words": tab2_words, "tab2_scales": tab2_scales,
            "w1": w1, "w4_words": w4_words, "w4_scales": w4_scales,
            "offs": offs, "offs2": offs2}

def reference(tab_words, tab_scales, tab2_words, tab2_scales, w1, w4_words, w4_scales, offs, offs2):
    v = unpack_weight(tab_words, tab_scales, "e4m3")[:, unstriped(offs)]
    v2 = unpack_weight(tab2_words, tab2_scales, "e4m3")[:, unstriped(offs2)]
    w4 = unpack_weight(w4_words, w4_scales, "e2m1")
    a = w4.T @ v
    b = mxq(f64(w1), 0, "e4m3").T @ v
    h = a * np.tanh(b)
    y = v2.T @ mxq(h, 0, "e4m3")
    x = 1.0 - y
    return 1.0 / (1.0 + x * x)

@@ -1,0 +1,243 @@
+from contextlib import ExitStack
+
+import concourse.mybir as mybir
+from concourse.masks import make_identity
+
+K, H, T, S, T2, S2 = 1536, 1024, 2048, 512, 2048, 1024
+FLOPS = 2 * (2 * K * H * S + H * S2 * S)
+
+F32 = mybir.dt.float32
+BF16 = mybir.dt.bfloat16
+I32 = mybir.dt.int32
+U32 = mybir.dt.uint32
+U16 = mybir.dt.uint16
+U8 = mybir.dt.uint8
+FP8X4 = mybir.dt.float8_e4m3fn_x4
+FP4X4 = mybir.dt.float4_e2m1fn_x4
+ACT = mybir.ActivationFunctionType
+ALU = mybir.AluOpType
+
+P = 128
+PASS = 512
+KP = K // PASS
+HP = H // PASS
+QT = S // P
+LT = S2 // P
+
+
+def tile_list_ligand_cauchy_affinity_kernel(
+    tc, tab_words, tab_scales, tab2_words, tab2_scales, w1, w4_words, w4_scales, offs, offs2, out
+):
+    nc = tc.nc
+    with ExitStack() as ctx:
+        keep = ctx.enter_context(tc.tile_pool(name="keep", bufs=1))
+        ring = ctx.enter_context(tc.tile_pool(name="ring", bufs=3))
+        psum = ctx.enter_context(tc.psum_pool(name="psum", bufs=1))
+
+        offs_sb = keep.tile([P, S // 16], U16, name="offs_sb")
+        offs2_sb = keep.tile([P, S2 // 16], U16, name="offs2_sb")
+        tabw = [keep.tile([P, T], I32, name="tabw%d" % a, align_bytes=64) for a in range(KP)]
+        tab2w = [keep.tile([P, T2], I32, name="tab2w%d" % b, align_bytes=64) for b in range(HP)]
+        tabs = keep.tile([P, KP, T], U8, name="tabs", align_bytes=64)
+        tab2s = keep.tile([P, T2], U8, name="tab2s", align_bytes=64)
+        w4w = keep.tile([P, KP, 2 * H], U8, name="w4w", align_bytes=64)
+        w4s = keep.tile([P, KP, H], U8, name="w4s", align_bytes=64)
+        vw = keep.tile([P, KP, S], U32, name="vw", align_bytes=64)
+        vs = keep.tile([P, KP, S], U8, name="vs", align_bytes=64)
+        v2w = keep.tile([P, HP, S2], U32, name="v2w", align_bytes=64)
+        v2s = keep.tile([P, S2], U8, name="v2s", align_bytes=64)
+        w1raw = {}
+        w1c = {}
+        w1s = {}
+        for b in range(HP):
+            for a in range(KP):
+                w1raw[b, a] = keep.tile([P, 4, PASS], F32, name="w1raw%d%d" % (b, a), align_bytes=64)
+                w1c[b, a] = keep.tile([P, PASS], U32, name="w1c%d%d" % (b, a), align_bytes=64)
+                w1s[b, a] = keep.tile([P, PASS], U8, name="w1s%d%d" % (b, a), align_bytes=64)
+        hq = [keep.tile([P, S, 4], BF16, name="hq%d" % b, align_bytes=64) for b in range(HP)]
+        hc = keep.tile([P, HP, S], U32, name="hc", align_bytes=64)
+        hs = keep.tile([P, HP, S], U8, name="hs", align_bytes=64)
+        ident = keep.tile([P, P], F32, name="ident", align_bytes=64)
+        banks = [psum.tile([P, 512], F32, name="bank%d" % i) for i in range(8)]
+
+        def load_w1(b, a, c0=0, c1=PASS):
+            rows = w1[PASS * a : PASS * (a + 1), PASS * b + c0 : PASS * b + c1]
+            nc.sync.dma_start(out=w1raw[b, a][:, :, c0:c1], in_=rows.rearrange("(p j) c -> p j c", j=4))
+
+        def load_words(tile, words):
+            nc.sync.dma_start(out=tile[:], in_=words.rearrange("p t i -> p (t i)").bitcast(I32))
+
+        def load_w4(b):
+            cols = slice(2 * PASS * b, 2 * PASS * (b + 1))
+            nc.sync.dma_start(
+                out=w4w[:, :, cols].bitcast(I32), in_=w4_words[:, :, cols].bitcast(I32).rearrange("a p c -> p a c")
+            )
+
+        def load_planes(tile, scales):
+            for q in range(4):
+                nc.sync.dma_start(
+                    out=tile[32 * q : 32 * q + 4, :, :].bitcast(I32),
+                    in_=scales[:, 4 * q : 4 * q + 4, :].bitcast(I32).rearrange("a r t -> r a t"),
+                )
+
+        nc.gpsimd.memset(tabs[:, 0, :].bitcast(I32), 0)
+        nc.vector.memset(tabs[:, 1:3, :].bitcast(I32), 0)
+        nc.vector.memset(tab2s[:].bitcast(I32), 0)
+        nc.vector.memset(w4s[:].bitcast(I32), 0)
+        make_identity(nc, ident[:])
+
+        load_w1(0, 0, 0, 256)
+        nc.sync.dma_start(offs_sb[:], offs)
+        load_planes(tabs, tab_scales)
+        load_w1(0, 0, 256, 512)
+        load_words(tabw[0], tab_words[0])
+        nc.sync.dma_start(offs2_sb[:], offs2)
+        for q in range(4):
+            nc.sync.dma_start(
+                out=tab2s[32 * q + 8 : 32 * q + 16, :].bitcast(I32),
+                in_=tab2_scales[:, 4 * q : 4 * q + 4, :].bitcast(I32),
+            )
+        load_w1(0, 1)
+        load_w1(0, 2)
+        load_words(tabw[1], tab_words[1])
+        load_w1(1, 0)
+        load_planes(w4s, w4_scales)
+        load_words(tabw[2], tab_words[2])
+        load_w4(0)
+        load_w1(1, 1)
+        load_w1(1, 2, 0, 256)
+        load_w1(1, 2, 256, 512)
+        load_w4(1)
+        load_words(tab2w[0], tab2_words[0])
+        load_words(tab2w[1], tab2_words[1])
+
+        def cast_w1(b, a, shares):
+            grouped = ring.tile([P, PASS, 4], BF16, name="grouped", align_bytes=64)
+            dst = grouped[:].rearrange("p (c i) t -> p c t i", i=4)
+            src = w1raw[b, a][:].rearrange("p t (c i) -> p c t i", i=4)
+            for engine, lo, hi in shares:
+                cols = slice(lo // 4, hi // 4)
+                if engine == "scalar":
+                    nc.scalar.copy(out=dst[:, cols], in_=src[:, cols])
+                else:
+                    nc.vector.tensor_copy(out=dst[:, cols], in_=src[:, cols])
+            return grouped
+
+        def quant_w1(b, a, grouped):
+            nc.vector.quantize_mx(
+                out=w1c[b, a][:].bitcast(FP8X4),
+                scales=w1s[b, a][:],
+                in_=grouped[:].rearrange("p c t -> p (c t)"),
+            )
+
+        def gather_v(a):
+            nc.vector.tensor_copy(vw[:, a, :], tabw[a][:].bitcast(U32).indirect(offs_sb[:]))
+
+        def mm_b(b, a):
+            for j in range(QT):
+                cols = slice(P * j, P * (j + 1))
+                nc.tensor.matmul_mx(
+                    out=banks[4 + j][:],
+                    lhsT=vw[:, a, cols].bitcast(FP8X4),
+                    lhsT_scale=vs[:, a, cols],
+                    rhs=w1c[b, a][:].bitcast(FP8X4),
+                    rhs_scale=w1s[b, a][:],
+                    start=(a == 0),
+                    stop=(a == KP - 1),
+                )
+
+        def mm_a(b):
+            for j in range(QT):
+                cols = slice(P * j, P * (j + 1))
+                for a in range(KP):
+                    nc.tensor.matmul_mx(
+                        out=banks[j][:],
+                        lhsT=vw[:, a, cols].bitcast(FP8X4),
+                        lhsT_scale=vs[:, a, cols],
+                        rhs=w4w[:, a, 2 * PASS * b : 2 * PASS * (b + 1)].bitcast(FP4X4),
+                        rhs_scale=w4s[:, a, PASS * b : PASS * (b + 1)],
+                        start=(a == 0),
+                        stop=(a == KP - 1),
+                    )
+
+        def gate(b):
+            order = "q (p u e) -> q u p e"
+            hb = {}
+            for j in range(QT + 1):
+                if j < QT:
+                    th = ring.tile([P, 2, P, 2], F32, name="th", align_bytes=64)
+                    nc.scalar.activation(th[:], banks[4 + j][:].rearrange(order, u=2, e=2), ACT.Tanh)
+                    hb[j] = ring.tile([P, 2, P, 2], BF16, name="hb", align_bytes=64)
+                    nc.vector.tensor_tensor(hb[j][:], banks[j][:].rearrange(order, u=2, e=2), th[:], ALU.mult)
+                if j > 0:
+                    i = j - 1
+                    words = hb[i][:].rearrange("q u p e -> q (u p e)").bitcast(F32)
+                    for u in range(2):
+                        nc.tensor.transpose(banks[i][:, P * u : P * (u + 1)], words[:, P * u : P * (u + 1)], ident[:])
+                    dst = hq[b][:, P * i : P * (i + 1), :]
+                    nc.scalar.copy(
+                        out=dst.bitcast(F32),
+                        in_=banks[i][:, 0 : 2 * P].rearrange("p (u n) -> p n u", u=2),
+                    )
+                    nc.vector.quantize_mx(
+                        out=hc[:, b, P * i : P * (i + 1)].bitcast(FP8X4),
+                        scales=hs[:, b, P * i : P * (i + 1)],
+                        in_=dst.rearrange("p n t -> p (n t)"),
+                    )
+
+        whole = [("scalar", 0, PASS)]
+        g = cast_w1(0, 0, [("scalar", 0, 256), ("scalar", 256, 512)])
+        for a in range(KP):
+            nc.vector.tensor_copy(vs[:, a, :], tabs[:, a, :].indirect(offs_sb[:]))
+        quant_w1(0, 0, g)
+        gather_v(0)
+        mm_b(0, 0)
+        nc.vector.tensor_copy(v2s[:], tab2s[:].indirect(offs2_sb[:]))
+        g = cast_w1(0, 1, whole)
+        quant_w1(0, 1, g)
+        g = cast_w1(0, 2, whole)
+        gather_v(1)
+        mm_b(0, 1)
+        quant_w1(0, 2, g)
+        g = cast_w1(1, 0, whole)
+        gather_v(2)
+        mm_b(0, 2)
+        mm_a(0)
+        quant_w1(1, 0, g)
+        gate(0)
+        mm_b(1, 0)
+        g = cast_w1(1, 1, [("vector", 0, PASS)])
+        quant_w1(1, 1, g)
+        mm_b(1, 1)
+        g = cast_w1(1, 2, [("scalar", 0, 256), ("vector", 256, 512)])
+        quant_w1(1, 2, g)
+        mm_b(1, 2)
+        mm_a(1)
+        gate(1)
+
+        for i in range(LT):
+            cols = slice(P * i, P * (i + 1))
+            if i % 2 == 0:
+                for b in range(HP):
+                    nc.vector.tensor_copy(
+                        v2w[:, b, P * i : P * (i + 2)],
+                        tab2w[b][:].bitcast(U32).indirect(offs2_sb[:, 8 * i : 8 * (i + 2)]),
+                    )
+            bank = banks[(4 + i) % 8]
+            for b in range(HP):
+                nc.tensor.matmul_mx(
+                    out=bank[:],
+                    lhsT=v2w[:, b, cols].bitcast(FP8X4),
+                    lhsT_scale=v2s[8 + 4 * b : P, cols],
+                    rhs=hc[:, b, :].bitcast(FP8X4),
+                    rhs_scale=hs[:, b, :],
+                    start=(b == 0),
+                    stop=(b == HP - 1),
+                )
+            sq = ring.tile([P, S], F32, name="sq")
+            nc.scalar.activation(sq[:], bank[:], ACT.Square, bias=1.0, scale=-1.0)
+            rs = ring.tile([P, S], F32, name="rs")
+            nc.scalar.activation(rs[:], sq[:], ACT.Abs_reciprocal_sqrt, bias=1.0)
+            res = ring.tile([P, S], F32, name="res", bufs=4)
+            nc.vector.tensor_tensor(res[:], rs[:], rs[:], ALU.mult)
+            nc.sync.dma_start(out=out[cols, :], in_=res[:])

@@ -31,7 +31,7 @@ def tile_list_ligand_cauchy_affinity_kernel(
     nc = tc.nc
     with ExitStack() as ctx:
         keep = ctx.enter_context(tc.tile_pool(name="keep", bufs=1))
-        ring = ctx.enter_context(tc.tile_pool(name="ring", bufs=3))
+        ring = ctx.enter_context(tc.tile_pool(name="ring", bufs=4))
         psum = ctx.enter_context(tc.psum_pool(name="psum", bufs=1))
 
         offs_sb = keep.tile([P, S // 16], U16, name="offs_sb")
@@ -44,20 +44,22 @@ def tile_list_ligand_cauchy_affinity_kernel(
         w4s = keep.tile([P, KP, H], U8, name="w4s", align_bytes=64)
         vw = keep.tile([P, KP, S], U32, name="vw", align_bytes=64)
         vs = keep.tile([P, KP, S], U8, name="vs", align_bytes=64)
-        v2w = keep.tile([P, HP, S2], U32, name="v2w", align_bytes=64)
         v2s = keep.tile([P, S2], U8, name="v2s", align_bytes=64)
         w1raw = {}
+        w1bf = {}
         w1c = {}
         w1s = {}
         for b in range(HP):
             for a in range(KP):
                 w1raw[b, a] = keep.tile([P, 4, PASS], F32, name="w1raw%d%d" % (b, a), align_bytes=64)
+                w1bf[b, a] = keep.tile([P, PASS, 4], BF16, name="w1bf%d%d" % (b, a), align_bytes=64)
                 w1c[b, a] = keep.tile([P, PASS], U32, name="w1c%d%d" % (b, a), align_bytes=64)
                 w1s[b, a] = keep.tile([P, PASS], U8, name="w1s%d%d" % (b, a), align_bytes=64)
         hq = [keep.tile([P, S, 4], BF16, name="hq%d" % b, align_bytes=64) for b in range(HP)]
         hc = keep.tile([P, HP, S], U32, name="hc", align_bytes=64)
         hs = keep.tile([P, HP, S], U8, name="hs", align_bytes=64)
         ident = keep.tile([P, P], F32, name="ident", align_bytes=64)
+        warm = keep.tile([P, 8], F32, name="warm")
         banks = [psum.tile([P, 512], F32, name="bank%d" % i) for i in range(8)]
 
         def load_w1(b, a, c0=0, c1=PASS):
@@ -67,71 +69,84 @@ def tile_list_ligand_cauchy_affinity_kernel(
         def load_words(tile, words):
             nc.sync.dma_start(out=tile[:], in_=words.rearrange("p t i -> p (t i)").bitcast(I32))
 
-        def load_w4(b):
-            cols = slice(2 * PASS * b, 2 * PASS * (b + 1))
+        def load_w4(b0, b1):
+            cols = slice(2 * PASS * b0, 2 * PASS * b1)
             nc.sync.dma_start(
                 out=w4w[:, :, cols].bitcast(I32), in_=w4_words[:, :, cols].bitcast(I32).rearrange("a p c -> p a c")
             )
 
         def load_planes(tile, scales):
-            for q in range(4):
+            for r in range(4):
                 nc.sync.dma_start(
-                    out=tile[32 * q : 32 * q + 4, :, :].bitcast(I32),
-                    in_=scales[:, 4 * q : 4 * q + 4, :].bitcast(I32).rearrange("a r t -> r a t"),
+                    out=tile[r:P:32, :, :].bitcast(I32),
+                    in_=scales[:, r:16:4, :].bitcast(I32).rearrange("a q t -> q a t"),
+                )
+
+        def load_packed_planes():
+            for q in range(4):
+                nc.gpsimd.dma_start(
+                    out=tab2s[32 * q + 8 : 32 * q + 16, :].bitcast(I32),
+                    in_=tab2_scales[:, 4 * q : 4 * q + 4, :].bitcast(I32),
                 )
 
         nc.gpsimd.memset(tabs[:, 0, :].bitcast(I32), 0)
         nc.vector.memset(tabs[:, 1:3, :].bitcast(I32), 0)
         nc.vector.memset(tab2s[:].bitcast(I32), 0)
         nc.vector.memset(w4s[:].bitcast(I32), 0)
+        load_packed_planes()
         make_identity(nc, ident[:])
 
-        load_w1(0, 0, 0, 256)
-        nc.sync.dma_start(offs_sb[:], offs)
+        load_w1(0, 0)
         load_planes(tabs, tab_scales)
-        load_w1(0, 0, 256, 512)
+        nc.sync.dma_start(offs_sb[:], offs)
         load_words(tabw[0], tab_words[0])
         nc.sync.dma_start(offs2_sb[:], offs2)
-        for q in range(4):
-            nc.sync.dma_start(
-                out=tab2s[32 * q + 8 : 32 * q + 16, :].bitcast(I32),
-                in_=tab2_scales[:, 4 * q : 4 * q + 4, :].bitcast(I32),
-            )
         load_w1(0, 1)
-        load_w1(0, 2)
         load_words(tabw[1], tab_words[1])
-        load_w1(1, 0)
-        load_planes(w4s, w4_scales)
+        load_w1(0, 2)
         load_words(tabw[2], tab_words[2])
-        load_w4(0)
+        load_planes(w4s, w4_scales)
+        load_w4(0, 2)
+        load_w1(1, 0)
         load_w1(1, 1)
         load_w1(1, 2, 0, 256)
         load_w1(1, 2, 256, 512)
-        load_w4(1)
         load_words(tab2w[0], tab2_words[0])
         load_words(tab2w[1], tab2_words[1])
 
         def cast_w1(b, a, shares):
-            grouped = ring.tile([P, PASS, 4], BF16, name="grouped", align_bytes=64)
-            dst = grouped[:].rearrange("p (c i) t -> p c t i", i=4)
+            dst = w1bf[b, a][:].rearrange("p (c i) t -> p c t i", i=4)
             src = w1raw[b, a][:].rearrange("p t (c i) -> p c t i", i=4)
             for engine, lo, hi in shares:
                 cols = slice(lo // 4, hi // 4)
                 if engine == "scalar":
                     nc.scalar.copy(out=dst[:, cols], in_=src[:, cols])
-                else:
+                elif engine == "vector":
                     nc.vector.tensor_copy(out=dst[:, cols], in_=src[:, cols])
-            return grouped
+                else:
+                    nc.gpsimd.tensor_scalar(dst[:, cols], src[:, cols], 1.0, 0.0, ALU.mult, ALU.add)
 
-        def quant_w1(b, a, grouped):
-            nc.vector.quantize_mx(
-                out=w1c[b, a][:].bitcast(FP8X4),
-                scales=w1s[b, a][:],
-                in_=grouped[:].rearrange("p c t -> p (c t)"),
-            )
+        def quant_w1(b, a, pieces):
+            n = PASS // pieces
+            for s in range(pieces):
+                cols = slice(n * s, n * (s + 1))
+                nc.vector.quantize_mx(
+                    out=w1c[b, a][:, cols].bitcast(FP8X4),
+                    scales=w1s[b, a][:, cols],
+                    in_=w1bf[b, a][:, cols, :].rearrange("p c t -> p (c t)"),
+                )
 
-        def gather_v(a):
-            nc.vector.tensor_copy(vw[:, a, :], tabw[a][:].bitcast(U32).indirect(offs_sb[:]))
+        def gather_query_scales():
+            for a in range(KP):
+                nc.vector.tensor_copy(vs[:, a, :], tabs[:, a, :].indirect(offs_sb[:]))
+
+        def gather_v(a, pieces):
+            n = S // pieces
+            for s in range(pieces):
+                nc.vector.tensor_copy(
+                    vw[:, a, n * s : n * (s + 1)],
+                    tabw[a][:].bitcast(U32).indirect(offs_sb[:, n // 16 * s : n // 16 * (s + 1)]),
+                )
 
         def mm_b(b, a):
             for j in range(QT):
@@ -160,84 +175,105 @@ def tile_list_ligand_cauchy_affinity_kernel(
                         stop=(a == KP - 1),
                     )
 
-        def gate(b):
+        def gate(b, copy_on):
             order = "q (p u e) -> q u p e"
             hb = {}
-            for j in range(QT + 1):
-                if j < QT:
-                    th = ring.tile([P, 2, P, 2], F32, name="th", align_bytes=64)
-                    nc.scalar.activation(th[:], banks[4 + j][:].rearrange(order, u=2, e=2), ACT.Tanh)
-                    hb[j] = ring.tile([P, 2, P, 2], BF16, name="hb", align_bytes=64)
-                    nc.vector.tensor_tensor(hb[j][:], banks[j][:].rearrange(order, u=2, e=2), th[:], ALU.mult)
-                if j > 0:
-                    i = j - 1
-                    words = hb[i][:].rearrange("q u p e -> q (u p e)").bitcast(F32)
-                    for u in range(2):
-                        nc.tensor.transpose(banks[i][:, P * u : P * (u + 1)], words[:, P * u : P * (u + 1)], ident[:])
-                    dst = hq[b][:, P * i : P * (i + 1), :]
-                    nc.scalar.copy(
-                        out=dst.bitcast(F32),
-                        in_=banks[i][:, 0 : 2 * P].rearrange("p (u n) -> p n u", u=2),
-                    )
-                    nc.vector.quantize_mx(
-                        out=hc[:, b, P * i : P * (i + 1)].bitcast(FP8X4),
-                        scales=hs[:, b, P * i : P * (i + 1)],
-                        in_=dst.rearrange("p n t -> p (n t)"),
-                    )
+            th = {}
+            for j in range(QT):
+                th[j] = ring.tile([P, 2, P, 2], F32, name="th", align_bytes=64)
+                nc.scalar.activation(th[j][:], banks[4 + j][:].rearrange(order, u=2, e=2), ACT.Tanh)
+                hb[j] = ring.tile([P, 2, P, 2], BF16, name="hb", align_bytes=64)
+                nc.vector.tensor_tensor(hb[j][:], banks[j][:].rearrange(order, u=2, e=2), th[j][:], ALU.mult)
+            if b == HP - 1 and False:
+                nc.scalar.activation(warm[:, 0:2], th[QT - 1][:, 0, 0, :], ACT.Abs_reciprocal_sqrt, bias=1.0, scale=0.5)
+            for i in range(QT):
+                tb = banks[i + 0]
+                words = hb[i][:].rearrange("q u p e -> q (u p e)").bitcast(F32)
+                for u in range(2):
+                    nc.tensor.transpose(tb[:, P * u : P * (u + 1)], words[:, P * u : P * (u + 1)], ident[:])
+                dst = hq[b][:, P * i : P * (i + 1), :]
+                src = tb[:, 0 : 2 * P].rearrange("p (u n) -> p n u", u=2)
+                if copy_on[i] == "S":
+                    nc.scalar.copy(out=dst.bitcast(F32), in_=src)
+                else:
+                    nc.vector.tensor_copy(out=dst.bitcast(F32), in_=src)
+                nc.vector.quantize_mx(
+                    out=hc[:, b, P * i : P * (i + 1)].bitcast(FP8X4),
+                    scales=hs[:, b, P * i : P * (i + 1)],
+                    in_=dst.rearrange("p n t -> p (n t)"),
+                )
+            if b == HP - 1 and True:
+                nc.scalar.activation(warm[:, 0:2], hq[b][:, S - 1, 0:2], ACT.Abs_reciprocal_sqrt, bias=1.0, scale=0.0)
 
-        whole = [("scalar", 0, PASS)]
-        g = cast_w1(0, 0, [("scalar", 0, 256), ("scalar", 256, 512)])
-        for a in range(KP):
-            nc.vector.tensor_copy(vs[:, a, :], tabs[:, a, :].indirect(offs_sb[:]))
-        quant_w1(0, 0, g)
-        gather_v(0)
-        mm_b(0, 0)
+        gather_query_scales()
+        gather_v(0, 1)
+        gather_v(1, 1)
+        gather_v(2, 2)
+        cast_w1(0, 0, [("scalar", 0, 512)])
+        cast_w1(0, 1, [("scalar", 0, 512)])
+        cast_w1(0, 2, [("scalar", 0, 512)])
+        cast_w1(1, 0, [("scalar", 0, 384), ("vector", 384, 512)])
+        cast_w1(1, 1, [("scalar", 0, 128), ("vector", 128, 256), ("scalar", 256, 384), ("vector", 384, 512)])
+        cast_w1(1, 2, [("scalar", 0, 96), ("vector", 96, 256), ("scalar", 256, 352), ("vector", 352, 512)])
+        quant_w1(0, 0, 1)
+        quant_w1(0, 1, 1)
+        quant_w1(0, 2, 1)
+        quant_w1(1, 0, 1)
+        quant_w1(1, 1, 1)
+        quant_w1(1, 2, 2)
         nc.vector.tensor_copy(v2s[:], tab2s[:].indirect(offs2_sb[:]))
-        g = cast_w1(0, 1, whole)
-        quant_w1(0, 1, g)
-        g = cast_w1(0, 2, whole)
-        gather_v(1)
+        mm_b(0, 0)
         mm_b(0, 1)
-        quant_w1(0, 2, g)
-        g = cast_w1(1, 0, whole)
-        gather_v(2)
         mm_b(0, 2)
         mm_a(0)
-        quant_w1(1, 0, g)
-        gate(0)
+        gate(0, "SVSV")
         mm_b(1, 0)
-        g = cast_w1(1, 1, [("vector", 0, PASS)])
-        quant_w1(1, 1, g)
         mm_b(1, 1)
-        g = cast_w1(1, 2, [("scalar", 0, 256), ("vector", 256, 512)])
-        quant_w1(1, 2, g)
         mm_b(1, 2)
         mm_a(1)
-        gate(1)
+        gate(1, "SVSS")
 
+        v2w = {}
+        sq = {}
         for i in range(LT):
             cols = slice(P * i, P * (i + 1))
             if i % 2 == 0:
+                sq_pair = ring.tile([P, 2, S], F32, name="sq_pair", bufs=3)
+                rs_pair = ring.tile([P, 2, S], F32, name="rs_pair", bufs=3)
                 for b in range(HP):
+                    v2w[b] = ring.tile([P, 2 * P], U32, name="v2w%d" % b, align_bytes=64, bufs=2)
                     nc.vector.tensor_copy(
-                        v2w[:, b, P * i : P * (i + 2)],
-                        tab2w[b][:].bitcast(U32).indirect(offs2_sb[:, 8 * i : 8 * (i + 2)]),
+                        v2w[b][:], tab2w[b][:].bitcast(U32).indirect(offs2_sb[:, 8 * i : 8 * (i + 2)])
                     )
             bank = banks[(4 + i) % 8]
-            for b in range(HP):
+            passes = (0, 1)
+            for b in passes:
                 nc.tensor.matmul_mx(
                     out=bank[:],
-                    lhsT=v2w[:, b, cols].bitcast(FP8X4),
+                    lhsT=v2w[b][:, P * (i % 2) : P * (i % 2 + 1)].bitcast(FP8X4),
                     lhsT_scale=v2s[8 + 4 * b : P, cols],
                     rhs=hc[:, b, :].bitcast(FP8X4),
                     rhs_scale=hs[:, b, :],
-                    start=(b == 0),
-                    stop=(b == HP - 1),
+                    start=(b == passes[0]),
+                    stop=(b == passes[1]),
                 )
-            sq = ring.tile([P, S], F32, name="sq")
-            nc.scalar.activation(sq[:], bank[:], ACT.Square, bias=1.0, scale=-1.0)
-            rs = ring.tile([P, S], F32, name="rs")
-            nc.scalar.activation(rs[:], sq[:], ACT.Abs_reciprocal_sqrt, bias=1.0)
-            res = ring.tile([P, S], F32, name="res", bufs=4)
-            nc.vector.tensor_tensor(res[:], rs[:], rs[:], ALU.mult)
-            nc.sync.dma_start(out=out[cols, :], in_=res[:])
+            if "AAABAAAA"[i] == "A":
+                nc.scalar.activation(sq_pair[:, i % 2, :], bank[:], ACT.Square, bias=1.0, scale=-1.0)
+            else:
+                dist = ring.tile([P, S], F32, name="dist", bufs=2)
+                nc.vector.tensor_scalar(dist[:], bank[:], -1.0, None, ALU.add)
+                nc.vector.scalar_tensor_tensor(sq_pair[:, i % 2, :], bank[:], -1.0, dist[:], ALU.add, ALU.mult)
+            wide = "1100"[i // 2] == "1"
+            if wide and i % 2 == 0:
+                continue
+            done = slice(0, 2) if wide else slice(i % 2, i % 2 + 1)
+            nc.scalar.activation(rs_pair[:, done, :], sq_pair[:, done, :], ACT.Abs_reciprocal_sqrt, bias=1.0)
+            for x in range(done.start, done.stop):
+                row0 = P * (i - i % 2 + x)
+                pieces = 2 if row0 == S2 - P and True else 1
+                res = ring.tile([P, S], F32, name="res", bufs=8)
+                n = S // pieces
+                for s in range(pieces):
+                    part = slice(n * s, n * (s + 1))
+                    nc.vector.tensor_tensor(res[:, part], rs_pair[:, x, part], rs_pair[:, x, part], ALU.mult)
+                    nc.sync.dma_start(out=out[row0 : row0 + P, part], in_=res[:, part])

@@ -23,6 +23,8 @@ KP = K // PASS
 HP = H // PASS
 QT = S // P
 LT = S2 // P
+RQ = 256
+NQ = H // RQ
 
 
 def tile_list_ligand_cauchy_affinity_kernel(
@@ -40,39 +42,44 @@ def tile_list_ligand_cauchy_affinity_kernel(
         tab2w = [keep.tile([P, T2], I32, name="tab2w%d" % b, align_bytes=64) for b in range(HP)]
         tabs = keep.tile([P, KP, T], U8, name="tabs", align_bytes=64)
         tab2s = keep.tile([P, T2], U8, name="tab2s", align_bytes=64)
-        w4w = keep.tile([P, KP, 2 * H], U8, name="w4w", align_bytes=64)
+        w4w = [keep.tile([P, KP, 2 * PASS], U8, name="w4w%d" % b, align_bytes=64) for b in range(HP)]
         w4s = keep.tile([P, KP, H], U8, name="w4s", align_bytes=64)
-        vw = keep.tile([P, KP, S], U32, name="vw", align_bytes=64)
-        vs = keep.tile([P, KP, S], U8, name="vs", align_bytes=64)
+        vw = [keep.tile([P, S], U32, name="vw%d" % a, align_bytes=64) for a in range(KP)]
+        vs = [keep.tile([P, S], U8, name="vs%d" % a, align_bytes=64) for a in range(KP)]
         v2s = keep.tile([P, S2], U8, name="v2s", align_bytes=64)
         w1raw = {}
         w1bf = {}
         w1c = {}
         w1s = {}
-        for b in range(HP):
+        for q in range(NQ):
             for a in range(KP):
-                w1raw[b, a] = keep.tile([P, 4, PASS], F32, name="w1raw%d%d" % (b, a), align_bytes=64)
-                w1bf[b, a] = keep.tile([P, PASS, 4], BF16, name="w1bf%d%d" % (b, a), align_bytes=64)
-                w1c[b, a] = keep.tile([P, PASS], U32, name="w1c%d%d" % (b, a), align_bytes=64)
-                w1s[b, a] = keep.tile([P, PASS], U8, name="w1s%d%d" % (b, a), align_bytes=64)
-        hq = [keep.tile([P, S, 4], BF16, name="hq%d" % b, align_bytes=64) for b in range(HP)]
-        hc = keep.tile([P, HP, S], U32, name="hc", align_bytes=64)
-        hs = keep.tile([P, HP, S], U8, name="hs", align_bytes=64)
+                w1raw[q, a] = keep.tile([P, 4, RQ], F32, name="w1raw%d%d" % (q, a), align_bytes=64)
+                w1bf[q, a] = keep.tile([P, RQ, 4], BF16, name="w1bf%d%d" % (q, a), align_bytes=64)
+                w1c[q, a] = keep.tile([P, RQ], U32, name="w1c%d%d" % (q, a), align_bytes=64)
+                w1s[q, a] = keep.tile([P, RQ], U8, name="w1s%d%d" % (q, a), align_bytes=64)
+        hb = {}
+        hq = {}
+        for b in range(HP):
+            for g in range(2):
+                hb[b, g] = keep.tile([P, 2, 2, 2, 64, 2], BF16, name="hb%d%d" % (b, g), align_bytes=64)
+                hq[b, g] = keep.tile([P, 2 * P, 4], BF16, name="hq%d%d" % (b, g), align_bytes=64)
+        hc = [keep.tile([P, S], U32, name="hc%d" % b, align_bytes=64) for b in range(HP)]
+        hs = [keep.tile([P, S], U8, name="hs%d" % b, align_bytes=64) for b in range(HP)]
         ident = keep.tile([P, P], F32, name="ident", align_bytes=64)
         warm = keep.tile([P, 8], F32, name="warm")
         banks = [psum.tile([P, 512], F32, name="bank%d" % i) for i in range(8)]
 
-        def load_w1(b, a, c0=0, c1=PASS):
-            rows = w1[PASS * a : PASS * (a + 1), PASS * b + c0 : PASS * b + c1]
-            nc.sync.dma_start(out=w1raw[b, a][:, :, c0:c1], in_=rows.rearrange("(p j) c -> p j c", j=4))
+        def load_w1(q, a):
+            rows = w1[PASS * a : PASS * (a + 1), RQ * q : RQ * (q + 1)]
+            nc.sync.dma_start(out=w1raw[q, a][:], in_=rows.rearrange("(p j) c -> p j c", j=4))
 
         def load_words(tile, words):
             nc.sync.dma_start(out=tile[:], in_=words.rearrange("p t i -> p (t i)").bitcast(I32))
 
-        def load_w4(b0, b1):
-            cols = slice(2 * PASS * b0, 2 * PASS * b1)
+        def load_w4(b):
+            cols = slice(2 * PASS * b, 2 * PASS * (b + 1))
             nc.sync.dma_start(
-                out=w4w[:, :, cols].bitcast(I32), in_=w4_words[:, :, cols].bitcast(I32).rearrange("a p c -> p a c")
+                out=w4w[b][:].bitcast(I32), in_=w4_words[:, :, cols].bitcast(I32).rearrange("a p c -> p a c")
             )
 
         def load_planes(tile, scales):
@@ -100,180 +107,190 @@ def tile_list_ligand_cauchy_affinity_kernel(
         load_planes(tabs, tab_scales)
         nc.sync.dma_start(offs_sb[:], offs)
         load_words(tabw[0], tab_words[0])
+        load_planes(w4s, w4_scales)
+        load_w4(0)
+        load_words(tabw[1], tab_words[1])
         nc.sync.dma_start(offs2_sb[:], offs2)
         load_w1(0, 1)
-        load_words(tabw[1], tab_words[1])
-        load_w1(0, 2)
         load_words(tabw[2], tab_words[2])
-        load_planes(w4s, w4_scales)
-        load_w4(0, 2)
+        load_w1(0, 2)
         load_w1(1, 0)
         load_w1(1, 1)
-        load_w1(1, 2, 0, 256)
-        load_w1(1, 2, 256, 512)
+        load_w1(1, 2)
+        load_w4(1)
+        load_w1(2, 0)
+        load_w1(2, 1)
+        load_w1(2, 2)
+        load_w1(3, 0)
+        load_w1(3, 1)
+        load_w1(3, 2)
         load_words(tab2w[0], tab2_words[0])
         load_words(tab2w[1], tab2_words[1])
 
-        def cast_w1(b, a, shares):
-            dst = w1bf[b, a][:].rearrange("p (c i) t -> p c t i", i=4)
-            src = w1raw[b, a][:].rearrange("p t (c i) -> p c t i", i=4)
+        def cast_w1(q, a, shares):
+            dst = w1bf[q, a][:].rearrange("p (c i) t -> p c t i", i=4)
+            src = w1raw[q, a][:].rearrange("p t (c i) -> p c t i", i=4)
             for engine, lo, hi in shares:
                 cols = slice(lo // 4, hi // 4)
                 if engine == "scalar":
                     nc.scalar.copy(out=dst[:, cols], in_=src[:, cols])
-                elif engine == "vector":
-                    nc.vector.tensor_copy(out=dst[:, cols], in_=src[:, cols])
                 else:
-                    nc.gpsimd.tensor_scalar(dst[:, cols], src[:, cols], 1.0, 0.0, ALU.mult, ALU.add)
+                    nc.vector.tensor_copy(out=dst[:, cols], in_=src[:, cols])
 
-        def quant_w1(b, a, pieces):
-            n = PASS // pieces
-            for s in range(pieces):
-                cols = slice(n * s, n * (s + 1))
-                nc.vector.quantize_mx(
-                    out=w1c[b, a][:, cols].bitcast(FP8X4),
-                    scales=w1s[b, a][:, cols],
-                    in_=w1bf[b, a][:, cols, :].rearrange("p c t -> p (c t)"),
-                )
-
-        def gather_query_scales():
-            for a in range(KP):
-                nc.vector.tensor_copy(vs[:, a, :], tabs[:, a, :].indirect(offs_sb[:]))
+        def quant_w1(q, a):
+            nc.vector.quantize_mx(
+                out=w1c[q, a][:].bitcast(FP8X4),
+                scales=w1s[q, a][:],
+                in_=w1bf[q, a][:].rearrange("p c t -> p (c t)"),
+            )
 
         def gather_v(a, pieces):
             n = S // pieces
             for s in range(pieces):
                 nc.vector.tensor_copy(
-                    vw[:, a, n * s : n * (s + 1)],
+                    vw[a][:, n * s : n * (s + 1)],
                     tabw[a][:].bitcast(U32).indirect(offs_sb[:, n // 16 * s : n // 16 * (s + 1)]),
                 )
 
-        def mm_b(b, a):
+        def bank_a(q, g):
+            return banks[2 * (q % 2) + g]
+
+        def bank_b(q, g):
+            return banks[4 + 2 * (q % 2) + g]
+
+        def bank_t(g):
+            return banks[2 + g]
+
+        def mm_b(q, a):
             for j in range(QT):
                 cols = slice(P * j, P * (j + 1))
                 nc.tensor.matmul_mx(
-                    out=banks[4 + j][:],
-                    lhsT=vw[:, a, cols].bitcast(FP8X4),
-                    lhsT_scale=vs[:, a, cols],
-                    rhs=w1c[b, a][:].bitcast(FP8X4),
-                    rhs_scale=w1s[b, a][:],
-                    start=(a == 0),
-                    stop=(a == KP - 1),
+                    out=bank_b(q, j // 2)[:, RQ * (j % 2) : RQ * (j % 2 + 1)],
+                    lhsT=vw[a][:, cols].bitcast(FP8X4),
+                    lhsT_scale=vs[a][:, cols],
+                    rhs=w1c[q, a][:].bitcast(FP8X4),
+                    rhs_scale=w1s[q, a][:],
+                    start=(a == 0 and j % 2 == 0),
+                    stop=(a == KP - 1 and j % 2 == 1),
                 )
 
-        def mm_a(b):
+        def mm_a(q, a):
             for j in range(QT):
                 cols = slice(P * j, P * (j + 1))
-                for a in range(KP):
+                for x in range(2):
+                    c0 = RQ * (q % 2) + P * x
                     nc.tensor.matmul_mx(
-                        out=banks[j][:],
-                        lhsT=vw[:, a, cols].bitcast(FP8X4),
-                        lhsT_scale=vs[:, a, cols],
-                        rhs=w4w[:, a, 2 * PASS * b : 2 * PASS * (b + 1)].bitcast(FP4X4),
-                        rhs_scale=w4s[:, a, PASS * b : PASS * (b + 1)],
-                        start=(a == 0),
-                        stop=(a == KP - 1),
+                        out=bank_a(q, j // 2)[:, RQ * (j % 2) + P * x : RQ * (j % 2) + P * (x + 1)],
+                        lhsT=vw[a][:, cols].bitcast(FP8X4),
+                        lhsT_scale=vs[a][:, cols],
+                        rhs=w4w[q // 2][:, a, 2 * c0 : 2 * (c0 + P)].bitcast(FP4X4),
+                        rhs_scale=w4s[:, a, RQ * q + P * x : RQ * q + P * (x + 1)],
+                        start=(a == 0 and j % 2 == 0 and x == 0),
+                        stop=(a == KP - 1 and j % 2 == 1 and x == 1),
                     )
 
-        def gate(b, copy_on):
-            order = "q (p u e) -> q u p e"
-            hb = {}
-            th = {}
-            for j in range(QT):
-                th[j] = ring.tile([P, 2, P, 2], F32, name="th", align_bytes=64)
-                nc.scalar.activation(th[j][:], banks[4 + j][:].rearrange(order, u=2, e=2), ACT.Tanh)
-                hb[j] = ring.tile([P, 2, P, 2], BF16, name="hb", align_bytes=64)
-                nc.vector.tensor_tensor(hb[j][:], banks[j][:].rearrange(order, u=2, e=2), th[j][:], ALU.mult)
-            if b == HP - 1 and False:
-                nc.scalar.activation(warm[:, 0:2], th[QT - 1][:, 0, 0, :], ACT.Abs_reciprocal_sqrt, bias=1.0, scale=0.5)
-            for i in range(QT):
-                tb = banks[i + 0]
-                words = hb[i][:].rearrange("q u p e -> q (u p e)").bitcast(F32)
-                for u in range(2):
-                    nc.tensor.transpose(tb[:, P * u : P * (u + 1)], words[:, P * u : P * (u + 1)], ident[:])
-                dst = hq[b][:, P * i : P * (i + 1), :]
-                src = tb[:, 0 : 2 * P].rearrange("p (u n) -> p n u", u=2)
-                if copy_on[i] == "S":
-                    nc.scalar.copy(out=dst.bitcast(F32), in_=src)
-                else:
-                    nc.vector.tensor_copy(out=dst.bitcast(F32), in_=src)
-                nc.vector.quantize_mx(
-                    out=hc[:, b, P * i : P * (i + 1)].bitcast(FP8X4),
-                    scales=hs[:, b, P * i : P * (i + 1)],
-                    in_=dst.rearrange("p n t -> p (n t)"),
+        last_th = {}
+
+        def gate(q):
+            order = "n (j p u e) -> n u j p e"
+            for g in range(2):
+                th = ring.tile([P, 2, 2, 64, 2], F32, name="th", align_bytes=64)
+                last_th[g] = th
+                nc.scalar.activation(th[:], bank_b(q, g)[:].rearrange(order, j=2, u=2, e=2), ACT.Tanh)
+                nc.vector.tensor_tensor(
+                    hb[q // 2, g][:, :, :, q % 2, :, :],
+                    bank_a(q, g)[:].rearrange(order, j=2, u=2, e=2),
+                    th[:],
+                    ALU.mult,
                 )
-            if b == HP - 1 and True:
-                nc.scalar.activation(warm[:, 0:2], hq[b][:, S - 1, 0:2], ACT.Abs_reciprocal_sqrt, bias=1.0, scale=0.0)
 
-        gather_query_scales()
-        gather_v(0, 1)
-        gather_v(1, 1)
-        gather_v(2, 2)
-        cast_w1(0, 0, [("scalar", 0, 512)])
-        cast_w1(0, 1, [("scalar", 0, 512)])
-        cast_w1(0, 2, [("scalar", 0, 512)])
-        cast_w1(1, 0, [("scalar", 0, 384), ("vector", 384, 512)])
-        cast_w1(1, 1, [("scalar", 0, 128), ("vector", 128, 256), ("scalar", 256, 384), ("vector", 384, 512)])
-        cast_w1(1, 2, [("scalar", 0, 96), ("vector", 96, 256), ("scalar", 256, 352), ("vector", 352, 512)])
-        quant_w1(0, 0, 1)
-        quant_w1(0, 1, 1)
-        quant_w1(0, 2, 1)
-        quant_w1(1, 0, 1)
-        quant_w1(1, 1, 1)
-        quant_w1(1, 2, 2)
+        def turn(b, copy_on):
+            for g in range(2):
+                words = hb[b, g][:].rearrange("n u j c p e -> n (u j c p e)").bitcast(F32)
+                for j in range(2):
+                    for u in range(2):
+                        nc.tensor.transpose(
+                            bank_t(g)[:, P * (2 * j + u) : P * (2 * j + u + 1)],
+                            words[:, P * (2 * u + j) : P * (2 * u + j + 1)],
+                            ident[:],
+                        )
+                dst = hq[b, g][:].bitcast(F32).rearrange("p (j n) u -> p j n u", j=2)
+                src = bank_t(g)[:].rearrange("p (j u n) -> p j n u", j=2, u=2)
+                if copy_on[g] == "S":
+                    nc.scalar.copy(out=dst, in_=src)
+                else:
+                    nc.vector.tensor_copy(out=dst, in_=src)
+                nc.vector.quantize_mx(
+                    out=hc[b][:, 2 * P * g : 2 * P * (g + 1)].bitcast(FP8X4),
+                    scales=hs[b][:, 2 * P * g : 2 * P * (g + 1)],
+                    in_=hq[b, g][:].rearrange("p n t -> p (n t)"),
+                )
+
+        for a in range(KP):
+            nc.vector.tensor_copy(vs[a][:], tabs[:, a, :].indirect(offs_sb[:]))
+        for a in range(KP):
+            gather_v(a, 2 if a == KP - 1 else 1)
+            cast_w1(0, a, [("scalar", 0, RQ)] if a < KP - 1 else [("scalar", 0, 128), ("vector", 128, RQ)])
+            quant_w1(0, a)
+            mm_b(0, a)
+            mm_a(0, a)
         nc.vector.tensor_copy(v2s[:], tab2s[:].indirect(offs2_sb[:]))
-        mm_b(0, 0)
-        mm_b(0, 1)
-        mm_b(0, 2)
-        mm_a(0)
-        gate(0, "SVSV")
-        mm_b(1, 0)
-        mm_b(1, 1)
-        mm_b(1, 2)
-        mm_a(1)
-        gate(1, "SVSS")
+        shares = {1: [[("scalar", 0, RQ)], [("vector", 0, RQ)], [("scalar", 0, 96), ("vector", 96, RQ)]], 2: [[("scalar", 0, RQ)], [("vector", 0, RQ)], [("scalar", 0, 96), ("vector", 96, RQ)]], 3: [[("scalar", 0, RQ)], [("vector", 0, RQ)], [("scalar", 0, 96), ("vector", 96, RQ)]]}
+        for q in range(1, NQ):
+            gate(q - 1)
+            if q == 2:
+                turn(0, "SS")
+            for a in range(KP):
+                mm_a(q, a)
+            for a in range(KP):
+                cast_w1(q, a, shares[q][a])
+                quant_w1(q, a)
+                mm_b(q, a)
+        gate(NQ - 1)
+        nc.scalar.activation(warm[:, 0:2], last_th[1][:, 0, 0, 0, :], ACT.Abs_reciprocal_sqrt, bias=1.0, scale=0.5)
+        turn(1, "SS")
 
+        early = [keep.tile([P, 2 * P], U32, name="early%d" % x, align_bytes=64) for x in range(2)]
         v2w = {}
-        sq = {}
+
+        def gather_v2(b, pair):
+            if b == 0 and pair < 2:
+                v2w[b, pair] = early[pair]
+            else:
+                v2w[b, pair] = ring.tile([P, 2 * P], U32, name="v2w", align_bytes=64, bufs=2)
+            nc.vector.tensor_copy(
+                v2w[b, pair][:], tab2w[b][:].bitcast(U32).indirect(offs2_sb[:, 16 * pair : 16 * (pair + 1)])
+            )
+
         for i in range(LT):
             cols = slice(P * i, P * (i + 1))
             if i % 2 == 0:
-                sq_pair = ring.tile([P, 2, S], F32, name="sq_pair", bufs=3)
-                rs_pair = ring.tile([P, 2, S], F32, name="rs_pair", bufs=3)
                 for b in range(HP):
-                    v2w[b] = ring.tile([P, 2 * P], U32, name="v2w%d" % b, align_bytes=64, bufs=2)
-                    nc.vector.tensor_copy(
-                        v2w[b][:], tab2w[b][:].bitcast(U32).indirect(offs2_sb[:, 8 * i : 8 * (i + 2)])
-                    )
-            bank = banks[(4 + i) % 8]
-            passes = (0, 1)
-            for b in passes:
+                    gather_v2(b, i // 2)
+            bank = banks[(0, 1, 4, 5, 6, 7, 2, 3)[i]]
+            for b in range(HP):
                 nc.tensor.matmul_mx(
                     out=bank[:],
-                    lhsT=v2w[b][:, P * (i % 2) : P * (i % 2 + 1)].bitcast(FP8X4),
+                    lhsT=v2w[b, i // 2][:, P * (i % 2) : P * (i % 2 + 1)].bitcast(FP8X4),
                     lhsT_scale=v2s[8 + 4 * b : P, cols],
-                    rhs=hc[:, b, :].bitcast(FP8X4),
-                    rhs_scale=hs[:, b, :],
-                    start=(b == passes[0]),
-                    stop=(b == passes[1]),
+                    rhs=hc[b][:].bitcast(FP8X4),
+                    rhs_scale=hs[b][:],
+                    start=(b == 0),
+                    stop=(b == HP - 1),
                 )
-            if "AAABAAAA"[i] == "A":
-                nc.scalar.activation(sq_pair[:, i % 2, :], bank[:], ACT.Square, bias=1.0, scale=-1.0)
-            else:
+            sq = ring.tile([P, S], F32, name="sq", bufs=4)
+            rs = ring.tile([P, S], F32, name="rs", bufs=4)
+            res = ring.tile([P, S], F32, name="res", bufs=8)
+            if i in ():
                 dist = ring.tile([P, S], F32, name="dist", bufs=2)
                 nc.vector.tensor_scalar(dist[:], bank[:], -1.0, None, ALU.add)
-                nc.vector.scalar_tensor_tensor(sq_pair[:, i % 2, :], bank[:], -1.0, dist[:], ALU.add, ALU.mult)
-            wide = "1100"[i // 2] == "1"
-            if wide and i % 2 == 0:
-                continue
-            done = slice(0, 2) if wide else slice(i % 2, i % 2 + 1)
-            nc.scalar.activation(rs_pair[:, done, :], sq_pair[:, done, :], ACT.Abs_reciprocal_sqrt, bias=1.0)
-            for x in range(done.start, done.stop):
-                row0 = P * (i - i % 2 + x)
-                pieces = 2 if row0 == S2 - P and True else 1
-                res = ring.tile([P, S], F32, name="res", bufs=8)
-                n = S // pieces
-                for s in range(pieces):
-                    part = slice(n * s, n * (s + 1))
-                    nc.vector.tensor_tensor(res[:, part], rs_pair[:, x, part], rs_pair[:, x, part], ALU.mult)
-                    nc.sync.dma_start(out=out[row0 : row0 + P, part], in_=res[:, part])
+                nc.vector.scalar_tensor_tensor(sq[:], bank[:], -1.0, dist[:], ALU.add, ALU.mult)
+            else:
+                nc.scalar.activation(sq[:], bank[:], ACT.Square, bias=1.0, scale=-1.0)
+            nc.scalar.activation(rs[:], sq[:], ACT.Abs_reciprocal_sqrt, bias=1.0)
+            pieces = 2 if i == LT - 1 else 1
+            n = S // pieces
+            for s in range(pieces):
+                part = slice(n * s, n * (s + 1))
+                nc.vector.tensor_tensor(res[:, part], rs[:, part], rs[:, part], ALU.mult)
+                nc.sync.dma_start(out=out[P * i : P * (i + 1), part], in_=res[:, part])

@@ -91,7 +91,7 @@ def tile_list_ligand_cauchy_affinity_kernel(
 
         def load_packed_planes():
             for q in range(4):
-                nc.gpsimd.dma_start(
+                nc.sync.dma_start(
                     out=tab2s[32 * q + 8 : 32 * q + 16, :].bitcast(I32),
                     in_=tab2_scales[:, 4 * q : 4 * q + 4, :].bitcast(I32),
                 )
@@ -100,13 +100,13 @@ def tile_list_ligand_cauchy_affinity_kernel(
         nc.vector.memset(tabs[:, 1:3, :].bitcast(I32), 0)
         nc.vector.memset(tab2s[:].bitcast(I32), 0)
         nc.vector.memset(w4s[:].bitcast(I32), 0)
-        load_packed_planes()
         make_identity(nc, ident[:])
 
         load_w1(0, 0)
         load_planes(tabs, tab_scales)
         nc.sync.dma_start(offs_sb[:], offs)
         load_words(tabw[0], tab_words[0])
+        load_packed_planes()
         load_planes(w4s, w4_scales)
         load_w4(0)
         load_words(tabw[1], tab_words[1])

@@ -53,7 +53,7 @@ def tile_list_ligand_cauchy_affinity_kernel(
         w1s = {}
         for q in range(NQ):
             for a in range(KP):
-                w1raw[q, a] = keep.tile([P, 4, RQ], F32, name="w1raw%d%d" % (q, a), align_bytes=64)
+                w1raw[q, a] = keep.tile([P, 4, RQ], F32, name="w1raw%d%d" % (q, a), tag="w1raw%d%d" % (q, a), align_bytes=64)
                 w1bf[q, a] = keep.tile([P, RQ, 4], BF16, name="w1bf%d%d" % (q, a), align_bytes=64)
                 w1c[q, a] = keep.tile([P, RQ], U32, name="w1c%d%d" % (q, a), align_bytes=64)
                 w1s[q, a] = keep.tile([P, RQ], U8, name="w1s%d%d" % (q, a), align_bytes=64)
@@ -62,7 +62,7 @@ def tile_list_ligand_cauchy_affinity_kernel(
         for b in range(HP):
             for g in range(2):
                 hb[b, g] = keep.tile([P, 2, 2, 2, 64, 2], BF16, name="hb%d%d" % (b, g), align_bytes=64)
-                hq[b, g] = keep.tile([P, 2 * P, 4], BF16, name="hq%d%d" % (b, g), align_bytes=64)
+                hq[b, g] = keep.tile([P, 2 * P, 4], BF16, name="hq%d%d" % (b, g), tag="hq%d%d" % (b, g), align_bytes=64)
         hc = [keep.tile([P, S], U32, name="hc%d" % b, align_bytes=64) for b in range(HP)]
         hs = [keep.tile([P, S], U8, name="hs%d" % b, align_bytes=64) for b in range(HP)]
         ident = keep.tile([P, P], F32, name="ident", align_bytes=64)
@@ -91,7 +91,7 @@ def tile_list_ligand_cauchy_affinity_kernel(
 
         def load_packed_planes():
             for q in range(4):
-                nc.sync.dma_start(
+                nc.gpsimd.dma_start(
                     out=tab2s[32 * q + 8 : 32 * q + 16, :].bitcast(I32),
                     in_=tab2_scales[:, 4 * q : 4 * q + 4, :].bitcast(I32),
                 )
@@ -100,13 +100,13 @@ def tile_list_ligand_cauchy_affinity_kernel(
         nc.vector.memset(tabs[:, 1:3, :].bitcast(I32), 0)
         nc.vector.memset(tab2s[:].bitcast(I32), 0)
         nc.vector.memset(w4s[:].bitcast(I32), 0)
+        load_packed_planes()
         make_identity(nc, ident[:])
 
         load_w1(0, 0)
         load_planes(tabs, tab_scales)
         nc.sync.dma_start(offs_sb[:], offs)
         load_words(tabw[0], tab_words[0])
-        load_packed_planes()
         load_planes(w4s, w4_scales)
         load_w4(0)
         load_words(tabw[1], tab_words[1])
@@ -158,8 +158,8 @@ def tile_list_ligand_cauchy_affinity_kernel(
         def bank_b(q, g):
             return banks[4 + 2 * (q % 2) + g]
 
-        def bank_t(g):
-            return banks[2 + g]
+        def bank_t(b, g):
+            return banks[4 + 2 * b + g]
 
         def mm_b(q, a):
             for j in range(QT):
@@ -193,8 +193,15 @@ def tile_list_ligand_cauchy_affinity_kernel(
 
         def gate(q):
             order = "n (j p u e) -> n u j p e"
+            if q == NQ - 2:
+                held = keep.tile([P, 2, 2, 2, 64, 2], F32, name="held", tag="w1raw%d%d" % (NQ - 1, KP - 1), align_bytes=64)
             for g in range(2):
-                th = ring.tile([P, 2, 2, 64, 2], F32, name="th", align_bytes=64)
+                if q == NQ - 2:
+                    th = held[:, g]
+                elif q == NQ - 1 and g == 0:
+                    th = keep.tile([P, 2, 2, 64, 2], F32, name="th_last", tag="th_last", align_bytes=64)
+                else:
+                    th = ring.tile([P, 2, 2, 64, 2], F32, name="th", align_bytes=64)
                 last_th[g] = th
                 nc.scalar.activation(th[:], bank_b(q, g)[:].rearrange(order, j=2, u=2, e=2), ACT.Tanh)
                 nc.vector.tensor_tensor(
@@ -210,12 +217,12 @@ def tile_list_ligand_cauchy_affinity_kernel(
                 for j in range(2):
                     for u in range(2):
                         nc.tensor.transpose(
-                            bank_t(g)[:, P * (2 * j + u) : P * (2 * j + u + 1)],
+                            bank_t(b, g)[:, P * (2 * j + u) : P * (2 * j + u + 1)],
                             words[:, P * (2 * u + j) : P * (2 * u + j + 1)],
                             ident[:],
                         )
                 dst = hq[b, g][:].bitcast(F32).rearrange("p (j n) u -> p j n u", j=2)
-                src = bank_t(g)[:].rearrange("p (j u n) -> p j n u", j=2, u=2)
+                src = bank_t(b, g)[:].rearrange("p (j u n) -> p j n u", j=2, u=2)
                 if copy_on[g] == "S":
                     nc.scalar.copy(out=dst, in_=src)
                 else:
@@ -237,27 +244,26 @@ def tile_list_ligand_cauchy_affinity_kernel(
         nc.vector.tensor_copy(v2s[:], tab2s[:].indirect(offs2_sb[:]))
         shares = {1: [[("scalar", 0, RQ)], [("vector", 0, RQ)], [("scalar", 0, 96), ("vector", 96, RQ)]], 2: [[("scalar", 0, RQ)], [("vector", 0, RQ)], [("scalar", 0, 96), ("vector", 96, RQ)]], 3: [[("scalar", 0, RQ)], [("vector", 0, RQ)], [("scalar", 0, 96), ("vector", 96, RQ)]]}
         for q in range(1, NQ):
-            gate(q - 1)
-            if q == 2:
-                turn(0, "SS")
-            for a in range(KP):
-                mm_a(q, a)
+            if q < NQ - 1:
+                gate(q - 1)
             for a in range(KP):
                 cast_w1(q, a, shares[q][a])
                 quant_w1(q, a)
                 mm_b(q, a)
+            for a in range(KP):
+                mm_a(q, a)
+        gate(NQ - 2)
         gate(NQ - 1)
-        nc.scalar.activation(warm[:, 0:2], last_th[1][:, 0, 0, 0, :], ACT.Abs_reciprocal_sqrt, bias=1.0, scale=0.5)
-        turn(1, "SS")
+        turn(0, "SS")
+        turn(1, "SV")
+        nc.scalar.activation(warm[:, 0:2], hq[1, 0][:, 2 * P - 1, 0:2], ACT.Abs_reciprocal_sqrt, bias=1.0, scale=0.0)
 
-        early = [keep.tile([P, 2 * P], U32, name="early%d" % x, align_bytes=64) for x in range(2)]
         v2w = {}
+        first = keep.tile([P, HP, 2 * P], U32, name="first", tag="th_last", align_bytes=64)
+        late = keep.tile([P, LT // 2 - 1, HP, 2 * P], U32, name="late", tag="hq11", align_bytes=64)
 
         def gather_v2(b, pair):
-            if b == 0 and pair < 2:
-                v2w[b, pair] = early[pair]
-            else:
-                v2w[b, pair] = ring.tile([P, 2 * P], U32, name="v2w", align_bytes=64, bufs=2)
+            v2w[b, pair] = first[:, b, :] if pair == 0 else late[:, pair - 1, b, :]
             nc.vector.tensor_copy(
                 v2w[b, pair][:], tab2w[b][:].bitcast(U32).indirect(offs2_sb[:, 16 * pair : 16 * (pair + 1)])
             )
@@ -267,7 +273,7 @@ def tile_list_ligand_cauchy_affinity_kernel(
             if i % 2 == 0:
                 for b in range(HP):
                     gather_v2(b, i // 2)
-            bank = banks[(0, 1, 4, 5, 6, 7, 2, 3)[i]]
+            bank = banks[(2, 3, 0, 1, 4, 5, 6, 7)[i]]
             for b in range(HP):
                 nc.tensor.matmul_mx(
                     out=bank[:],
@@ -281,16 +287,16 @@ def tile_list_ligand_cauchy_affinity_kernel(
             sq = ring.tile([P, S], F32, name="sq", bufs=4)
             rs = ring.tile([P, S], F32, name="rs", bufs=4)
             res = ring.tile([P, S], F32, name="res", bufs=8)
-            if i in ():
+            if i in (6,):
                 dist = ring.tile([P, S], F32, name="dist", bufs=2)
                 nc.vector.tensor_scalar(dist[:], bank[:], -1.0, None, ALU.add)
                 nc.vector.scalar_tensor_tensor(sq[:], bank[:], -1.0, dist[:], ALU.add, ALU.mult)
             else:
                 nc.scalar.activation(sq[:], bank[:], ACT.Square, bias=1.0, scale=-1.0)
-            nc.scalar.activation(rs[:], sq[:], ACT.Abs_reciprocal_sqrt, bias=1.0)
             pieces = 2 if i == LT - 1 else 1
             n = S // pieces
             for s in range(pieces):
                 part = slice(n * s, n * (s + 1))
+                nc.scalar.activation(rs[:, part], sq[:, part], ACT.Abs_reciprocal_sqrt, bias=1.0)
                 nc.vector.tensor_tensor(res[:, part], rs[:, part], rs[:, part], ALU.mult)
                 nc.sync.dma_start(out=out[P * i : P * (i + 1), part], in_=res[:, part])

@@ -255,8 +255,8 @@ def tile_list_ligand_cauchy_affinity_kernel(
         gate(NQ - 2)
         gate(NQ - 1)
         turn(0, "SS")
-        turn(1, "SV")
-        nc.scalar.activation(warm[:, 0:2], hq[1, 0][:, 2 * P - 1, 0:2], ACT.Abs_reciprocal_sqrt, bias=1.0, scale=0.0)
+        turn(1, "SS")
+        nc.scalar.activation(warm[:, 0:2], bank_t(1, 1)[:, 0:2], ACT.Abs_reciprocal_sqrt, bias=1.0, scale=0.0)
 
         v2w = {}
         first = keep.tile([P, HP, 2 * P], U32, name="first", tag="th_last", align_bytes=64)

@@ -19,12 +19,21 @@ ALU = mybir.AluOpType
 
 P = 128
 PASS = 512
-KP = K // PASS
-HP = H // PASS
-QT = S // P
-LT = S2 // P
-RQ = 256
-NQ = H // RQ
+K_PASSES = K // PASS
+R_PASSES = H // PASS
+QUERY_TILES = S // P
+LIGAND_TILES = S2 // P
+QUARTER = 256
+QUARTERS = H // QUARTER
+LAST_PASS = K_PASSES - 1
+LAST_QUARTER = QUARTERS - 1
+RUN = 2
+LIGAND_PLANE = 8
+
+SCALAR_COLUMNS_FIRST = (QUARTER, QUARTER, 128)
+SCALAR_COLUMNS_LATER = (QUARTER, 0, 96)
+SQUARE_ON_VECTOR = 6
+Y_BANKS = (2, 3, 0, 1, 4, 5, 6, 7)
 
 
 def tile_list_ligand_cauchy_affinity_kernel(
@@ -38,43 +47,45 @@ def tile_list_ligand_cauchy_affinity_kernel(
 
         offs_sb = keep.tile([P, S // 16], U16, name="offs_sb")
         offs2_sb = keep.tile([P, S2 // 16], U16, name="offs2_sb")
-        tabw = [keep.tile([P, T], I32, name="tabw%d" % a, align_bytes=64) for a in range(KP)]
-        tab2w = [keep.tile([P, T2], I32, name="tab2w%d" % b, align_bytes=64) for b in range(HP)]
-        tabs = keep.tile([P, KP, T], U8, name="tabs", align_bytes=64)
+        tabw = [keep.tile([P, T], I32, name="tabw%d" % a, align_bytes=64) for a in range(K_PASSES)]
+        tab2w = [keep.tile([P, T2], I32, name="tab2w%d" % b, align_bytes=64) for b in range(R_PASSES)]
+        tabs = keep.tile([P, K_PASSES, T], U8, name="tabs", align_bytes=64)
         tab2s = keep.tile([P, T2], U8, name="tab2s", align_bytes=64)
-        w4w = [keep.tile([P, KP, 2 * PASS], U8, name="w4w%d" % b, align_bytes=64) for b in range(HP)]
-        w4s = keep.tile([P, KP, H], U8, name="w4s", align_bytes=64)
-        vw = [keep.tile([P, S], U32, name="vw%d" % a, align_bytes=64) for a in range(KP)]
-        vs = [keep.tile([P, S], U8, name="vs%d" % a, align_bytes=64) for a in range(KP)]
+        w4w = [keep.tile([P, K_PASSES, 2 * PASS], U8, name="w4w%d" % b, align_bytes=64) for b in range(R_PASSES)]
+        w4s = keep.tile([P, K_PASSES, H], U8, name="w4s", align_bytes=64)
+        vw = [keep.tile([P, S], U32, name="vw%d" % a, align_bytes=64) for a in range(K_PASSES)]
+        vs = [keep.tile([P, S], U8, name="vs%d" % a, align_bytes=64) for a in range(K_PASSES)]
         v2s = keep.tile([P, S2], U8, name="v2s", align_bytes=64)
         w1raw = {}
         w1bf = {}
         w1c = {}
         w1s = {}
-        for q in range(NQ):
-            for a in range(KP):
-                w1raw[q, a] = keep.tile([P, 4, RQ], F32, name="w1raw%d%d" % (q, a), tag="w1raw%d%d" % (q, a), align_bytes=64)
-                w1bf[q, a] = keep.tile([P, RQ, 4], BF16, name="w1bf%d%d" % (q, a), align_bytes=64)
-                w1c[q, a] = keep.tile([P, RQ], U32, name="w1c%d%d" % (q, a), align_bytes=64)
-                w1s[q, a] = keep.tile([P, RQ], U8, name="w1s%d%d" % (q, a), align_bytes=64)
+        for q in range(QUARTERS):
+            for a in range(K_PASSES):
+                name = "%d%d" % (q, a)
+                w1raw[q, a] = keep.tile([P, 4, QUARTER], F32, name="w1raw" + name, tag="w1raw" + name, align_bytes=64)
+                w1bf[q, a] = keep.tile([P, QUARTER, 4], BF16, name="w1bf" + name, align_bytes=64)
+                w1c[q, a] = keep.tile([P, QUARTER], U32, name="w1c" + name, align_bytes=64)
+                w1s[q, a] = keep.tile([P, QUARTER], U8, name="w1s" + name, align_bytes=64)
         hb = {}
         hq = {}
-        for b in range(HP):
+        for b in range(R_PASSES):
             for g in range(2):
-                hb[b, g] = keep.tile([P, 2, 2, 2, 64, 2], BF16, name="hb%d%d" % (b, g), align_bytes=64)
-                hq[b, g] = keep.tile([P, 2 * P, 4], BF16, name="hq%d%d" % (b, g), tag="hq%d%d" % (b, g), align_bytes=64)
-        hc = [keep.tile([P, S], U32, name="hc%d" % b, align_bytes=64) for b in range(HP)]
-        hs = [keep.tile([P, S], U8, name="hs%d" % b, align_bytes=64) for b in range(HP)]
+                name = "%d%d" % (b, g)
+                hb[b, g] = keep.tile([P, 2, 2, 2, 64, 2], BF16, name="hb" + name, align_bytes=64)
+                hq[b, g] = keep.tile([P, 2 * P, 4], BF16, name="hq" + name, tag="hq" + name, align_bytes=64)
+        hc = [keep.tile([P, S], U32, name="hc%d" % b, align_bytes=64) for b in range(R_PASSES)]
+        hs = [keep.tile([P, S], U8, name="hs%d" % b, align_bytes=64) for b in range(R_PASSES)]
         ident = keep.tile([P, P], F32, name="ident", align_bytes=64)
         warm = keep.tile([P, 8], F32, name="warm")
         banks = [psum.tile([P, 512], F32, name="bank%d" % i) for i in range(8)]
 
         def load_w1(q, a):
-            rows = w1[PASS * a : PASS * (a + 1), RQ * q : RQ * (q + 1)]
-            nc.sync.dma_start(out=w1raw[q, a][:], in_=rows.rearrange("(p j) c -> p j c", j=4))
+            rows = w1[PASS * a : PASS * (a + 1), QUARTER * q : QUARTER * (q + 1)]
+            nc.sync.dma_start(out=w1raw[q, a][:], in_=rows.rearrange("(p t) c -> p t c", t=4))
 
         def load_words(tile, words):
-            nc.sync.dma_start(out=tile[:], in_=words.rearrange("p t i -> p (t i)").bitcast(I32))
+            nc.sync.dma_start(out=tile[:], in_=words.rearrange("p c t -> p (c t)").bitcast(I32))
 
         def load_w4(b):
             cols = slice(2 * PASS * b, 2 * PASS * (b + 1))
@@ -83,24 +94,22 @@ def tile_list_ligand_cauchy_affinity_kernel(
             )
 
         def load_planes(tile, scales):
-            for r in range(4):
+            for row in range(4):
                 nc.sync.dma_start(
-                    out=tile[r:P:32, :, :].bitcast(I32),
-                    in_=scales[:, r:16:4, :].bitcast(I32).rearrange("a q t -> q a t"),
-                )
-
-        def load_packed_planes():
-            for q in range(4):
-                nc.gpsimd.dma_start(
-                    out=tab2s[32 * q + 8 : 32 * q + 16, :].bitcast(I32),
-                    in_=tab2_scales[:, 4 * q : 4 * q + 4, :].bitcast(I32),
+                    out=tile[row:P:32, :, :].bitcast(I32),
+                    in_=scales[:, row:16:4, :].bitcast(I32).rearrange("a n c -> n a c"),
                 )
 
         nc.gpsimd.memset(tabs[:, 0, :].bitcast(I32), 0)
-        nc.vector.memset(tabs[:, 1:3, :].bitcast(I32), 0)
+        nc.vector.memset(tabs[:, 1:K_PASSES, :].bitcast(I32), 0)
         nc.vector.memset(tab2s[:].bitcast(I32), 0)
         nc.vector.memset(w4s[:].bitcast(I32), 0)
-        load_packed_planes()
+        for quadrant in range(4):
+            first_row = 32 * quadrant + LIGAND_PLANE
+            nc.gpsimd.dma_start(
+                out=tab2s[first_row : first_row + 4 * R_PASSES, :].bitcast(I32),
+                in_=tab2_scales[:, 4 * quadrant : 4 * quadrant + 4, :].bitcast(I32),
+            )
         make_identity(nc, ident[:])
 
         load_w1(0, 0)
@@ -114,37 +123,31 @@ def tile_list_ligand_cauchy_affinity_kernel(
         load_w1(0, 1)
         load_words(tabw[2], tab_words[2])
         load_w1(0, 2)
-        load_w1(1, 0)
-        load_w1(1, 1)
-        load_w1(1, 2)
-        load_w4(1)
-        load_w1(2, 0)
-        load_w1(2, 1)
-        load_w1(2, 2)
-        load_w1(3, 0)
-        load_w1(3, 1)
-        load_w1(3, 2)
-        load_words(tab2w[0], tab2_words[0])
-        load_words(tab2w[1], tab2_words[1])
+        for q in range(1, QUARTERS):
+            if q == QUARTERS // 2:
+                load_w4(1)
+            for a in range(K_PASSES):
+                load_w1(q, a)
+        for b in range(R_PASSES):
+            load_words(tab2w[b], tab2_words[b])
 
-        def cast_w1(q, a, shares):
-            dst = w1bf[q, a][:].rearrange("p (c i) t -> p c t i", i=4)
-            src = w1raw[q, a][:].rearrange("p t (c i) -> p c t i", i=4)
-            for engine, lo, hi in shares:
-                cols = slice(lo // 4, hi // 4)
-                if engine == "scalar":
-                    nc.scalar.copy(out=dst[:, cols], in_=src[:, cols])
-                else:
-                    nc.vector.tensor_copy(out=dst[:, cols], in_=src[:, cols])
+        def round_w1(q, a, scalar_columns):
+            dst = w1bf[q, a][:].rearrange("p (c i) t -> p c t i", i=RUN)
+            src = w1raw[q, a][:].rearrange("p t (c i) -> p c t i", i=RUN)
+            cut = scalar_columns // RUN
+            if scalar_columns > 0:
+                nc.scalar.copy(out=dst[:, :cut], in_=src[:, :cut])
+            if scalar_columns < QUARTER:
+                nc.vector.tensor_copy(out=dst[:, cut:], in_=src[:, cut:])
 
-        def quant_w1(q, a):
+        def quantise_w1(q, a):
             nc.vector.quantize_mx(
                 out=w1c[q, a][:].bitcast(FP8X4),
                 scales=w1s[q, a][:],
                 in_=w1bf[q, a][:].rearrange("p c t -> p (c t)"),
             )
 
-        def gather_v(a, pieces):
+        def gather_queries(a, pieces):
             n = S // pieces
             for s in range(pieces):
                 nc.vector.tensor_copy(
@@ -158,51 +161,52 @@ def tile_list_ligand_cauchy_affinity_kernel(
         def bank_b(q, g):
             return banks[4 + 2 * (q % 2) + g]
 
-        def bank_t(b, g):
+        def bank_turn(b, g):
             return banks[4 + 2 * b + g]
 
-        def mm_b(q, a):
-            for j in range(QT):
+        def multiply_b(q, a):
+            for j in range(QUERY_TILES):
                 cols = slice(P * j, P * (j + 1))
                 nc.tensor.matmul_mx(
-                    out=bank_b(q, j // 2)[:, RQ * (j % 2) : RQ * (j % 2 + 1)],
+                    out=bank_b(q, j // 2)[:, QUARTER * (j % 2) : QUARTER * (j % 2 + 1)],
                     lhsT=vw[a][:, cols].bitcast(FP8X4),
                     lhsT_scale=vs[a][:, cols],
                     rhs=w1c[q, a][:].bitcast(FP8X4),
                     rhs_scale=w1s[q, a][:],
                     start=(a == 0 and j % 2 == 0),
-                    stop=(a == KP - 1 and j % 2 == 1),
+                    stop=(a == LAST_PASS and j % 2 == 1),
                 )
 
-        def mm_a(q, a):
-            for j in range(QT):
+        def multiply_a(q, a):
+            for j in range(QUERY_TILES):
                 cols = slice(P * j, P * (j + 1))
                 for x in range(2):
-                    c0 = RQ * (q % 2) + P * x
+                    in_half = QUARTER * (q % 2) + P * x
+                    in_bank = QUARTER * (j % 2) + P * x
+                    in_h = QUARTER * q + P * x
                     nc.tensor.matmul_mx(
-                        out=bank_a(q, j // 2)[:, RQ * (j % 2) + P * x : RQ * (j % 2) + P * (x + 1)],
+                        out=bank_a(q, j // 2)[:, in_bank : in_bank + P],
                         lhsT=vw[a][:, cols].bitcast(FP8X4),
                         lhsT_scale=vs[a][:, cols],
-                        rhs=w4w[q // 2][:, a, 2 * c0 : 2 * (c0 + P)].bitcast(FP4X4),
-                        rhs_scale=w4s[:, a, RQ * q + P * x : RQ * q + P * (x + 1)],
+                        rhs=w4w[q // 2][:, a, 2 * in_half : 2 * (in_half + P)].bitcast(FP4X4),
+                        rhs_scale=w4s[:, a, in_h : in_h + P],
                         start=(a == 0 and j % 2 == 0 and x == 0),
-                        stop=(a == KP - 1 and j % 2 == 1 and x == 1),
+                        stop=(a == LAST_PASS and j % 2 == 1 and x == 1),
                     )
 
-        last_th = {}
-
         def gate(q):
-            order = "n (j p u e) -> n u j p e"
-            if q == NQ - 2:
-                held = keep.tile([P, 2, 2, 2, 64, 2], F32, name="held", tag="w1raw%d%d" % (NQ - 1, KP - 1), align_bytes=64)
+            order = "n (j m u e) -> n u j m e"
+            if q == LAST_QUARTER - 1:
+                held = keep.tile(
+                    [P, 2, 2, 2, 64, 2], F32, name="held", tag="w1raw%d%d" % (LAST_QUARTER, LAST_PASS), align_bytes=64
+                )
             for g in range(2):
-                if q == NQ - 2:
+                if q == LAST_QUARTER - 1:
                     th = held[:, g]
-                elif q == NQ - 1 and g == 0:
+                elif q == LAST_QUARTER and g == 0:
                     th = keep.tile([P, 2, 2, 64, 2], F32, name="th_last", tag="th_last", align_bytes=64)
                 else:
                     th = ring.tile([P, 2, 2, 64, 2], F32, name="th", align_bytes=64)
-                last_th[g] = th
                 nc.scalar.activation(th[:], bank_b(q, g)[:].rearrange(order, j=2, u=2, e=2), ACT.Tanh)
                 nc.vector.tensor_tensor(
                     hb[q // 2, g][:, :, :, q % 2, :, :],
@@ -211,89 +215,84 @@ def tile_list_ligand_cauchy_affinity_kernel(
                     ALU.mult,
                 )
 
-        def turn(b, copy_on):
+        def turn(b):
             for g in range(2):
-                words = hb[b, g][:].rearrange("n u j c p e -> n (u j c p e)").bitcast(F32)
+                words = hb[b, g][:].rearrange("n u j c m e -> n (u j c m e)").bitcast(F32)
                 for j in range(2):
                     for u in range(2):
                         nc.tensor.transpose(
-                            bank_t(b, g)[:, P * (2 * j + u) : P * (2 * j + u + 1)],
+                            bank_turn(b, g)[:, P * (2 * j + u) : P * (2 * j + u + 1)],
                             words[:, P * (2 * u + j) : P * (2 * u + j + 1)],
                             ident[:],
                         )
-                dst = hq[b, g][:].bitcast(F32).rearrange("p (j n) u -> p j n u", j=2)
-                src = bank_t(b, g)[:].rearrange("p (j u n) -> p j n u", j=2, u=2)
-                if copy_on[g] == "S":
-                    nc.scalar.copy(out=dst, in_=src)
-                else:
-                    nc.vector.tensor_copy(out=dst, in_=src)
+                nc.scalar.copy(
+                    out=hq[b, g][:].bitcast(F32).rearrange("p (j n) u -> p j n u", j=2),
+                    in_=bank_turn(b, g)[:].rearrange("p (j u n) -> p j n u", j=2, u=2),
+                )
                 nc.vector.quantize_mx(
                     out=hc[b][:, 2 * P * g : 2 * P * (g + 1)].bitcast(FP8X4),
                     scales=hs[b][:, 2 * P * g : 2 * P * (g + 1)],
                     in_=hq[b, g][:].rearrange("p n t -> p (n t)"),
                 )
 
-        for a in range(KP):
+        for a in range(K_PASSES):
             nc.vector.tensor_copy(vs[a][:], tabs[:, a, :].indirect(offs_sb[:]))
-        for a in range(KP):
-            gather_v(a, 2 if a == KP - 1 else 1)
-            cast_w1(0, a, [("scalar", 0, RQ)] if a < KP - 1 else [("scalar", 0, 128), ("vector", 128, RQ)])
-            quant_w1(0, a)
-            mm_b(0, a)
-            mm_a(0, a)
+        for a in range(K_PASSES):
+            gather_queries(a, 2 if a == LAST_PASS else 1)
+            round_w1(0, a, SCALAR_COLUMNS_FIRST[a])
+            quantise_w1(0, a)
+            multiply_b(0, a)
+            multiply_a(0, a)
         nc.vector.tensor_copy(v2s[:], tab2s[:].indirect(offs2_sb[:]))
-        shares = {1: [[("scalar", 0, RQ)], [("vector", 0, RQ)], [("scalar", 0, 96), ("vector", 96, RQ)]], 2: [[("scalar", 0, RQ)], [("vector", 0, RQ)], [("scalar", 0, 96), ("vector", 96, RQ)]], 3: [[("scalar", 0, RQ)], [("vector", 0, RQ)], [("scalar", 0, 96), ("vector", 96, RQ)]]}
-        for q in range(1, NQ):
-            if q < NQ - 1:
+        for q in range(1, QUARTERS):
+            if q < LAST_QUARTER:
                 gate(q - 1)
-            for a in range(KP):
-                cast_w1(q, a, shares[q][a])
-                quant_w1(q, a)
-                mm_b(q, a)
-            for a in range(KP):
-                mm_a(q, a)
-        gate(NQ - 2)
-        gate(NQ - 1)
-        turn(0, "SS")
-        turn(1, "SS")
-        nc.scalar.activation(warm[:, 0:2], bank_t(1, 1)[:, 0:2], ACT.Abs_reciprocal_sqrt, bias=1.0, scale=0.0)
+            for a in range(K_PASSES):
+                round_w1(q, a, SCALAR_COLUMNS_LATER[a])
+                quantise_w1(q, a)
+                multiply_b(q, a)
+            for a in range(K_PASSES):
+                multiply_a(q, a)
+        gate(LAST_QUARTER - 1)
+        gate(LAST_QUARTER)
+        for b in range(R_PASSES):
+            turn(b)
+        nc.scalar.activation(warm[:, 0:2], bank_turn(1, 1)[:, 0:2], ACT.Abs_reciprocal_sqrt, bias=1.0, scale=0.0)
 
-        v2w = {}
-        first = keep.tile([P, HP, 2 * P], U32, name="first", tag="th_last", align_bytes=64)
-        late = keep.tile([P, LT // 2 - 1, HP, 2 * P], U32, name="late", tag="hq11", align_bytes=64)
+        first = keep.tile([P, R_PASSES, 2 * P], U32, name="first", tag="th_last", align_bytes=64)
+        late = keep.tile([P, LIGAND_TILES // 2 - 1, R_PASSES, 2 * P], U32, name="late", tag="hq11", align_bytes=64)
 
-        def gather_v2(b, pair):
-            v2w[b, pair] = first[:, b, :] if pair == 0 else late[:, pair - 1, b, :]
-            nc.vector.tensor_copy(
-                v2w[b, pair][:], tab2w[b][:].bitcast(U32).indirect(offs2_sb[:, 16 * pair : 16 * (pair + 1)])
-            )
+        def ligand_words(b, pair):
+            return first[:, b, :] if pair == 0 else late[:, pair - 1, b, :]
 
-        for i in range(LT):
-            cols = slice(P * i, P * (i + 1))
+        for i in range(LIGAND_TILES):
+            pair = i // 2
             if i % 2 == 0:
-                for b in range(HP):
-                    gather_v2(b, i // 2)
-            bank = banks[(2, 3, 0, 1, 4, 5, 6, 7)[i]]
-            for b in range(HP):
+                for b in range(R_PASSES):
+                    nc.vector.tensor_copy(
+                        ligand_words(b, pair), tab2w[b][:].bitcast(U32).indirect(offs2_sb[:, 16 * pair : 16 * (pair + 1)])
+                    )
+            bank = banks[Y_BANKS[i]]
+            for b in range(R_PASSES):
                 nc.tensor.matmul_mx(
                     out=bank[:],
-                    lhsT=v2w[b, i // 2][:, P * (i % 2) : P * (i % 2 + 1)].bitcast(FP8X4),
-                    lhsT_scale=v2s[8 + 4 * b : P, cols],
+                    lhsT=ligand_words(b, pair)[:, P * (i % 2) : P * (i % 2 + 1)].bitcast(FP8X4),
+                    lhsT_scale=v2s[LIGAND_PLANE + 4 * b : P, P * i : P * (i + 1)],
                     rhs=hc[b][:].bitcast(FP8X4),
                     rhs_scale=hs[b][:],
                     start=(b == 0),
-                    stop=(b == HP - 1),
+                    stop=(b == R_PASSES - 1),
                 )
             sq = ring.tile([P, S], F32, name="sq", bufs=4)
             rs = ring.tile([P, S], F32, name="rs", bufs=4)
-            res = ring.tile([P, S], F32, name="res", bufs=8)
-            if i in (6,):
+            res = ring.tile([P, S], F32, name="res", bufs=LIGAND_TILES)
+            if i == SQUARE_ON_VECTOR:
                 dist = ring.tile([P, S], F32, name="dist", bufs=2)
                 nc.vector.tensor_scalar(dist[:], bank[:], -1.0, None, ALU.add)
                 nc.vector.scalar_tensor_tensor(sq[:], bank[:], -1.0, dist[:], ALU.add, ALU.mult)
             else:
                 nc.scalar.activation(sq[:], bank[:], ACT.Square, bias=1.0, scale=-1.0)
-            pieces = 2 if i == LT - 1 else 1
+            pieces = 2 if i == LIGAND_TILES - 1 else 1
             n = S // pieces
             for s in range(pieces):
                 part = slice(n * s, n * (s + 1))

@@ -178,21 +178,18 @@ def tile_list_ligand_cauchy_affinity_kernel(
                 )
 
         def multiply_a(q, a):
+            in_half = QUARTER * (q % 2)
             for j in range(QUERY_TILES):
                 cols = slice(P * j, P * (j + 1))
-                for x in range(2):
-                    in_half = QUARTER * (q % 2) + P * x
-                    in_bank = QUARTER * (j % 2) + P * x
-                    in_h = QUARTER * q + P * x
-                    nc.tensor.matmul_mx(
-                        out=bank_a(q, j // 2)[:, in_bank : in_bank + P],
-                        lhsT=vw[a][:, cols].bitcast(FP8X4),
-                        lhsT_scale=vs[a][:, cols],
-                        rhs=w4w[q // 2][:, a, 2 * in_half : 2 * (in_half + P)].bitcast(FP4X4),
-                        rhs_scale=w4s[:, a, in_h : in_h + P],
-                        start=(a == 0 and j % 2 == 0 and x == 0),
-                        stop=(a == LAST_PASS and j % 2 == 1 and x == 1),
-                    )
+                nc.tensor.matmul_mx(
+                    out=bank_a(q, j // 2)[:, QUARTER * (j % 2) : QUARTER * (j % 2 + 1)],
+                    lhsT=vw[a][:, cols].bitcast(FP8X4),
+                    lhsT_scale=vs[a][:, cols],
+                    rhs=w4w[q // 2][:, a, 2 * in_half : 2 * (in_half + QUARTER)].bitcast(FP4X4),
+                    rhs_scale=w4s[:, a, QUARTER * q : QUARTER * (q + 1)],
+                    start=(a == 0 and j % 2 == 0),
+                    stop=(a == LAST_PASS and j % 2 == 1),
+                )
 
         def gate(q):
             order = "n (j m u e) -> n u j m e"

@@ -51,8 +51,13 @@ def tile_list_ligand_cauchy_affinity_kernel(
         tab2w = [keep.tile([P, T2], I32, name="tab2w%d" % b, align_bytes=64) for b in range(R_PASSES)]
         tabs = keep.tile([P, K_PASSES, T], U8, name="tabs", align_bytes=64)
         tab2s = keep.tile([P, T2], U8, name="tab2s", align_bytes=64)
-        w4w = [keep.tile([P, K_PASSES, 2 * PASS], U8, name="w4w%d" % b, align_bytes=64) for b in range(R_PASSES)]
-        w4s = keep.tile([P, K_PASSES, H], U8, name="w4s", align_bytes=64)
+        w4_cols = (slice(0, QUARTER), slice(QUARTER, H))
+        w4w = []
+        w4s = []
+        for i, cols in enumerate(w4_cols):
+            n = cols.stop - cols.start
+            w4w.append(keep.tile([P, K_PASSES, 2 * n], U8, name="w4w%d" % i, align_bytes=64))
+            w4s.append(keep.tile([P, K_PASSES, n], U8, name="w4s%d" % i, align_bytes=64))
         vw = [keep.tile([P, S], U32, name="vw%d" % a, align_bytes=64) for a in range(K_PASSES)]
         vs = [keep.tile([P, S], U8, name="vs%d" % a, align_bytes=64) for a in range(K_PASSES)]
         v2s = keep.tile([P, S2], U8, name="v2s", align_bytes=64)
@@ -88,10 +93,11 @@ def tile_list_ligand_cauchy_affinity_kernel(
             nc.sync.dma_start(out=tile[:], in_=words.rearrange("p c t -> p (c t)").bitcast(I32))
 
         def load_w4(b):
-            cols = slice(2 * PASS * b, 2 * PASS * (b + 1))
+            cols = slice(2 * w4_cols[b].start, 2 * w4_cols[b].stop)
             nc.sync.dma_start(
                 out=w4w[b][:].bitcast(I32), in_=w4_words[:, :, cols].bitcast(I32).rearrange("a p c -> p a c")
             )
+            load_planes(w4s[b], w4_scales[:, :, w4_cols[b]])
 
         def load_planes(tile, scales):
             for row in range(4):
@@ -103,7 +109,8 @@ def tile_list_ligand_cauchy_affinity_kernel(
         nc.gpsimd.memset(tabs[:, 0, :].bitcast(I32), 0)
         nc.vector.memset(tabs[:, 1:K_PASSES, :].bitcast(I32), 0)
         nc.vector.memset(tab2s[:].bitcast(I32), 0)
-        nc.vector.memset(w4s[:].bitcast(I32), 0)
+        for plane in w4s:
+            nc.vector.memset(plane[:].bitcast(I32), 0)
         for quadrant in range(4):
             first_row = 32 * quadrant + LIGAND_PLANE
             nc.gpsimd.dma_start(
@@ -116,7 +123,6 @@ def tile_list_ligand_cauchy_affinity_kernel(
         load_planes(tabs, tab_scales)
         nc.sync.dma_start(offs_sb[:], offs)
         load_words(tabw[0], tab_words[0])
-        load_planes(w4s, w4_scales)
         load_w4(0)
         load_words(tabw[1], tab_words[1])
         nc.sync.dma_start(offs2_sb[:], offs2)
@@ -124,10 +130,10 @@ def tile_list_ligand_cauchy_affinity_kernel(
         load_words(tabw[2], tab_words[2])
         load_w1(0, 2)
         for q in range(1, QUARTERS):
-            if q == QUARTERS // 2:
-                load_w4(1)
             for a in range(K_PASSES):
                 load_w1(q, a)
+                if q == 1 and a == 0:
+                    load_w4(1)
         for b in range(R_PASSES):
             load_words(tab2w[b], tab2_words[b])
 
@@ -178,15 +184,16 @@ def tile_list_ligand_cauchy_affinity_kernel(
                 )
 
         def multiply_a(q, a):
-            in_half = QUARTER * (q % 2)
+            piece = min(q, 1)
+            at = QUARTER * q - w4_cols[piece].start
             for j in range(QUERY_TILES):
                 cols = slice(P * j, P * (j + 1))
                 nc.tensor.matmul_mx(
                     out=bank_a(q, j // 2)[:, QUARTER * (j % 2) : QUARTER * (j % 2 + 1)],
                     lhsT=vw[a][:, cols].bitcast(FP8X4),
                     lhsT_scale=vs[a][:, cols],
-                    rhs=w4w[q // 2][:, a, 2 * in_half : 2 * (in_half + QUARTER)].bitcast(FP4X4),
-                    rhs_scale=w4s[:, a, QUARTER * q : QUARTER * (q + 1)],
+                    rhs=w4w[piece][:, a, 2 * at : 2 * (at + QUARTER)].bitcast(FP4X4),
+                    rhs_scale=w4s[piece][:, a, at : at + QUARTER],
                     start=(a == 0 and j % 2 == 0),
                     stop=(a == LAST_PASS and j % 2 == 1),
                 )

@@ -97,11 +97,10 @@ def tile_list_ligand_cauchy_affinity_kernel(
             nc.sync.dma_start(
                 out=w4w[b][:].bitcast(I32), in_=w4_words[:, :, cols].bitcast(I32).rearrange("a p c -> p a c")
             )
-            load_planes(w4s[b], w4_scales[:, :, w4_cols[b]])
 
-        def load_planes(tile, scales):
+        def load_planes(queue, tile, scales):
             for row in range(4):
-                nc.sync.dma_start(
+                queue.dma_start(
                     out=tile[row:P:32, :, :].bitcast(I32),
                     in_=scales[:, row:16:4, :].bitcast(I32).rearrange("a n c -> n a c"),
                 )
@@ -117,13 +116,15 @@ def tile_list_ligand_cauchy_affinity_kernel(
                 out=tab2s[first_row : first_row + 4 * R_PASSES, :].bitcast(I32),
                 in_=tab2_scales[:, 4 * quadrant : 4 * quadrant + 4, :].bitcast(I32),
             )
+        load_planes(nc.gpsimd, w4s[1], w4_scales[:, :, w4_cols[1]])
         make_identity(nc, ident[:])
 
         load_w1(0, 0)
-        load_planes(tabs, tab_scales)
+        load_planes(nc.sync, tabs, tab_scales)
         nc.sync.dma_start(offs_sb[:], offs)
         load_words(tabw[0], tab_words[0])
         load_w4(0)
+        load_planes(nc.sync, w4s[0], w4_scales[:, :, w4_cols[0]])
         load_words(tabw[1], tab_words[1])
         nc.sync.dma_start(offs2_sb[:], offs2)
         load_w1(0, 1)

@@ -32,7 +32,8 @@ LIGAND_PLANE = 8
 
 SCALAR_COLUMNS_FIRST = (QUARTER, QUARTER, 128)
 SCALAR_COLUMNS_LATER = (QUARTER, 0, 96)
-SQUARE_ON_VECTOR = 6
+SQUARE_ON_VECTOR = (4, 5)
+LAST_SQUARE_ON_GPSIMD = (0, 1, 2)
 Y_BANKS = (2, 3, 0, 1, 4, 5, 6, 7)
 
 
@@ -270,13 +271,13 @@ def tile_list_ligand_cauchy_affinity_kernel(
         def ligand_words(b, pair):
             return first[:, b, :] if pair == 0 else late[:, pair - 1, b, :]
 
+        for pair in range(LIGAND_TILES // 2):
+            for b in range(R_PASSES):
+                nc.vector.tensor_copy(
+                    ligand_words(b, pair), tab2w[b][:].bitcast(U32).indirect(offs2_sb[:, 16 * pair : 16 * (pair + 1)])
+                )
         for i in range(LIGAND_TILES):
             pair = i // 2
-            if i % 2 == 0:
-                for b in range(R_PASSES):
-                    nc.vector.tensor_copy(
-                        ligand_words(b, pair), tab2w[b][:].bitcast(U32).indirect(offs2_sb[:, 16 * pair : 16 * (pair + 1)])
-                    )
             bank = banks[Y_BANKS[i]]
             for b in range(R_PASSES):
                 nc.tensor.matmul_mx(
@@ -288,19 +289,28 @@ def tile_list_ligand_cauchy_affinity_kernel(
                     start=(b == 0),
                     stop=(b == R_PASSES - 1),
                 )
-            sq = ring.tile([P, S], F32, name="sq", bufs=4)
-            rs = ring.tile([P, S], F32, name="rs", bufs=4)
+
+        sq = [
+            keep.tile([P, S], F32, name="sq%d" % i, tag="w1raw%d%d" % (i // K_PASSES, i % K_PASSES), align_bytes=64)
+            for i in range(LIGAND_TILES)
+        ]
+        dist = {i: keep.tile([P, S], F32, name="dist%d" % i, align_bytes=64) for i in SQUARE_ON_VECTOR}
+        for i in SQUARE_ON_VECTOR:
+            nc.vector.tensor_scalar(dist[i][:], banks[Y_BANKS[i]][:], -1.0, None, ALU.add)
+        for i in SQUARE_ON_VECTOR:
+            nc.vector.scalar_tensor_tensor(sq[i][:], banks[Y_BANKS[i]][:], -1.0, dist[i][:], ALU.add, ALU.mult)
+        on_scalar = [i for i in range(LIGAND_TILES) if i not in SQUARE_ON_VECTOR]
+        for i in range(LIGAND_TILES):
+            if i < len(on_scalar):
+                j = on_scalar[i]
+                nc.scalar.activation(sq[j][:], banks[Y_BANKS[j]][:], ACT.Square, bias=1.0, scale=-1.0)
+            rs = ring.tile([P, S], F32, name="rs", bufs=6)
             res = ring.tile([P, S], F32, name="res", bufs=LIGAND_TILES)
-            if i == SQUARE_ON_VECTOR:
-                dist = ring.tile([P, S], F32, name="dist", bufs=2)
-                nc.vector.tensor_scalar(dist[:], bank[:], -1.0, None, ALU.add)
-                nc.vector.scalar_tensor_tensor(sq[:], bank[:], -1.0, dist[:], ALU.add, ALU.mult)
-            else:
-                nc.scalar.activation(sq[:], bank[:], ACT.Square, bias=1.0, scale=-1.0)
             pieces = 2 if i == LIGAND_TILES - 1 else 1
             n = S // pieces
             for s in range(pieces):
                 part = slice(n * s, n * (s + 1))
-                nc.scalar.activation(rs[:, part], sq[:, part], ACT.Abs_reciprocal_sqrt, bias=1.0)
-                nc.vector.tensor_tensor(res[:, part], rs[:, part], rs[:, part], ALU.mult)
+                nc.scalar.activation(rs[:, part], sq[i][:, part], ACT.Abs_reciprocal_sqrt, bias=1.0)
+                engine = nc.gpsimd if i in LAST_SQUARE_ON_GPSIMD else nc.vector
+                engine.tensor_tensor(res[:, part], rs[:, part], rs[:, part], ALU.mult)
                 nc.sync.dma_start(out=out[P * i : P * (i + 1), part], in_=res[:, part])

from contextlib import ExitStack

import concourse.mybir as mybir
from concourse.masks import make_identity

K, H, T, S, T2, S2 = 1536, 1024, 2048, 512, 2048, 1024
FLOPS = 2 * (2 * K * H * S + H * S2 * S)

F32 = mybir.dt.float32
BF16 = mybir.dt.bfloat16
I32 = mybir.dt.int32
U32 = mybir.dt.uint32
U16 = mybir.dt.uint16
U8 = mybir.dt.uint8
FP8X4 = mybir.dt.float8_e4m3fn_x4
FP4X4 = mybir.dt.float4_e2m1fn_x4
ACT = mybir.ActivationFunctionType
ALU = mybir.AluOpType

P = 128
PASS = 512
K_PASSES = K // PASS
R_PASSES = H // PASS
QUERY_TILES = S // P
LIGAND_TILES = S2 // P
QUARTER = 256
QUARTERS = H // QUARTER
LAST_PASS = K_PASSES - 1
LAST_QUARTER = QUARTERS - 1
RUN = 2
LIGAND_PLANE = 8

SCALAR_COLUMNS_FIRST = (QUARTER, QUARTER, 128)
SCALAR_COLUMNS_LATER = (QUARTER, 0, 96)
SQUARE_ON_VECTOR = (4, 5)
LAST_SQUARE_ON_GPSIMD = (0, 1, 2)
Y_BANKS = (2, 3, 0, 1, 4, 5, 6, 7)


def tile_list_ligand_cauchy_affinity_kernel(
    tc, tab_words, tab_scales, tab2_words, tab2_scales, w1, w4_words, w4_scales, offs, offs2, out
):
    nc = tc.nc
    with ExitStack() as ctx:
        keep = ctx.enter_context(tc.tile_pool(name="keep", bufs=1))
        ring = ctx.enter_context(tc.tile_pool(name="ring", bufs=4))
        psum = ctx.enter_context(tc.psum_pool(name="psum", bufs=1))

        offs_sb = keep.tile([P, S // 16], U16, name="offs_sb")
        offs2_sb = keep.tile([P, S2 // 16], U16, name="offs2_sb")
        tabw = [keep.tile([P, T], I32, name="tabw%d" % a, align_bytes=64) for a in range(K_PASSES)]
        tab2w = [keep.tile([P, T2], I32, name="tab2w%d" % b, align_bytes=64) for b in range(R_PASSES)]
        tabs = keep.tile([P, K_PASSES, T], U8, name="tabs", align_bytes=64)
        tab2s = keep.tile([P, T2], U8, name="tab2s", align_bytes=64)
        w4_cols = (slice(0, QUARTER), slice(QUARTER, H))
        w4w = []
        w4s = []
        for i, cols in enumerate(w4_cols):
            n = cols.stop - cols.start
            w4w.append(keep.tile([P, K_PASSES, 2 * n], U8, name="w4w%d" % i, align_bytes=64))
            w4s.append(keep.tile([P, K_PASSES, n], U8, name="w4s%d" % i, align_bytes=64))
        vw = [keep.tile([P, S], U32, name="vw%d" % a, align_bytes=64) for a in range(K_PASSES)]
        vs = [keep.tile([P, S], U8, name="vs%d" % a, align_bytes=64) for a in range(K_PASSES)]
        v2s = keep.tile([P, S2], U8, name="v2s", align_bytes=64)
        w1raw = {}
        w1bf = {}
        w1c = {}
        w1s = {}
        for q in range(QUARTERS):
            for a in range(K_PASSES):
                name = "%d%d" % (q, a)
                w1raw[q, a] = keep.tile([P, 4, QUARTER], F32, name="w1raw" + name, tag="w1raw" + name, align_bytes=64)
                w1bf[q, a] = keep.tile([P, QUARTER, 4], BF16, name="w1bf" + name, align_bytes=64)
                w1c[q, a] = keep.tile([P, QUARTER], U32, name="w1c" + name, align_bytes=64)
                w1s[q, a] = keep.tile([P, QUARTER], U8, name="w1s" + name, align_bytes=64)
        hb = {}
        hq = {}
        for b in range(R_PASSES):
            for g in range(2):
                name = "%d%d" % (b, g)
                hb[b, g] = keep.tile([P, 2, 2, 2, 64, 2], BF16, name="hb" + name, align_bytes=64)
                hq[b, g] = keep.tile([P, 2 * P, 4], BF16, name="hq" + name, tag="hq" + name, align_bytes=64)
        hc = [keep.tile([P, S], U32, name="hc%d" % b, align_bytes=64) for b in range(R_PASSES)]
        hs = [keep.tile([P, S], U8, name="hs%d" % b, align_bytes=64) for b in range(R_PASSES)]
        ident = keep.tile([P, P], F32, name="ident", align_bytes=64)
        warm = keep.tile([P, 8], F32, name="warm")
        banks = [psum.tile([P, 512], F32, name="bank%d" % i) for i in range(8)]

        def load_w1(q, a):
            rows = w1[PASS * a : PASS * (a + 1), QUARTER * q : QUARTER * (q + 1)]
            nc.sync.dma_start(out=w1raw[q, a][:], in_=rows.rearrange("(p t) c -> p t c", t=4))

        def load_words(tile, words):
            nc.sync.dma_start(out=tile[:], in_=words.rearrange("p c t -> p (c t)").bitcast(I32))

        def load_w4(b):
            cols = slice(2 * w4_cols[b].start, 2 * w4_cols[b].stop)
            nc.sync.dma_start(
                out=w4w[b][:].bitcast(I32), in_=w4_words[:, :, cols].bitcast(I32).rearrange("a p c -> p a c")
            )

        def load_planes(queue, tile, scales):
            for row in range(4):
                queue.dma_start(
                    out=tile[row:P:32, :, :].bitcast(I32),
                    in_=scales[:, row:16:4, :].bitcast(I32).rearrange("a n c -> n a c"),
                )

        nc.gpsimd.memset(tabs[:, 0, :].bitcast(I32), 0)
        nc.vector.memset(tabs[:, 1:K_PASSES, :].bitcast(I32), 0)
        nc.vector.memset(tab2s[:].bitcast(I32), 0)
        for plane in w4s:
            nc.vector.memset(plane[:].bitcast(I32), 0)
        for quadrant in range(4):
            first_row = 32 * quadrant + LIGAND_PLANE
            nc.gpsimd.dma_start(
                out=tab2s[first_row : first_row + 4 * R_PASSES, :].bitcast(I32),
                in_=tab2_scales[:, 4 * quadrant : 4 * quadrant + 4, :].bitcast(I32),
            )
        load_planes(nc.gpsimd, w4s[1], w4_scales[:, :, w4_cols[1]])
        make_identity(nc, ident[:])

        load_w1(0, 0)
        load_planes(nc.sync, tabs, tab_scales)
        nc.sync.dma_start(offs_sb[:], offs)
        load_words(tabw[0], tab_words[0])
        load_w4(0)
        load_planes(nc.sync, w4s[0], w4_scales[:, :, w4_cols[0]])
        load_words(tabw[1], tab_words[1])
        nc.sync.dma_start(offs2_sb[:], offs2)
        load_w1(0, 1)
        load_words(tabw[2], tab_words[2])
        load_w1(0, 2)
        for q in range(1, QUARTERS):
            for a in range(K_PASSES):
                load_w1(q, a)
                if q == 1 and a == 0:
                    load_w4(1)
        for b in range(R_PASSES):
            load_words(tab2w[b], tab2_words[b])

        def round_w1(q, a, scalar_columns):
            dst = w1bf[q, a][:].rearrange("p (c i) t -> p c t i", i=RUN)
            src = w1raw[q, a][:].rearrange("p t (c i) -> p c t i", i=RUN)
            cut = scalar_columns // RUN
            if scalar_columns > 0:
                nc.scalar.copy(out=dst[:, :cut], in_=src[:, :cut])
            if scalar_columns < QUARTER:
                nc.vector.tensor_copy(out=dst[:, cut:], in_=src[:, cut:])

        def quantise_w1(q, a):
            nc.vector.quantize_mx(
                out=w1c[q, a][:].bitcast(FP8X4),
                scales=w1s[q, a][:],
                in_=w1bf[q, a][:].rearrange("p c t -> p (c t)"),
            )

        def gather_queries(a, pieces):
            n = S // pieces
            for s in range(pieces):
                nc.vector.tensor_copy(
                    vw[a][:, n * s : n * (s + 1)],
                    tabw[a][:].bitcast(U32).indirect(offs_sb[:, n // 16 * s : n // 16 * (s + 1)]),
                )

        def bank_a(q, g):
            return banks[2 * (q % 2) + g]

        def bank_b(q, g):
            return banks[4 + 2 * (q % 2) + g]

        def bank_turn(b, g):
            return banks[4 + 2 * b + g]

        def multiply_b(q, a):
            for j in range(QUERY_TILES):
                cols = slice(P * j, P * (j + 1))
                nc.tensor.matmul_mx(
                    out=bank_b(q, j // 2)[:, QUARTER * (j % 2) : QUARTER * (j % 2 + 1)],
                    lhsT=vw[a][:, cols].bitcast(FP8X4),
                    lhsT_scale=vs[a][:, cols],
                    rhs=w1c[q, a][:].bitcast(FP8X4),
                    rhs_scale=w1s[q, a][:],
                    start=(a == 0 and j % 2 == 0),
                    stop=(a == LAST_PASS and j % 2 == 1),
                )

        def multiply_a(q, a):
            piece = min(q, 1)
            at = QUARTER * q - w4_cols[piece].start
            for j in range(QUERY_TILES):
                cols = slice(P * j, P * (j + 1))
                nc.tensor.matmul_mx(
                    out=bank_a(q, j // 2)[:, QUARTER * (j % 2) : QUARTER * (j % 2 + 1)],
                    lhsT=vw[a][:, cols].bitcast(FP8X4),
                    lhsT_scale=vs[a][:, cols],
                    rhs=w4w[piece][:, a, 2 * at : 2 * (at + QUARTER)].bitcast(FP4X4),
                    rhs_scale=w4s[piece][:, a, at : at + QUARTER],
                    start=(a == 0 and j % 2 == 0),
                    stop=(a == LAST_PASS and j % 2 == 1),
                )

        def gate(q):
            order = "n (j m u e) -> n u j m e"
            if q == LAST_QUARTER - 1:
                held = keep.tile(
                    [P, 2, 2, 2, 64, 2], F32, name="held", tag="w1raw%d%d" % (LAST_QUARTER, LAST_PASS), align_bytes=64
                )
            for g in range(2):
                if q == LAST_QUARTER - 1:
                    th = held[:, g]
                elif q == LAST_QUARTER and g == 0:
                    th = keep.tile([P, 2, 2, 64, 2], F32, name="th_last", tag="th_last", align_bytes=64)
                else:
                    th = ring.tile([P, 2, 2, 64, 2], F32, name="th", align_bytes=64)
                nc.scalar.activation(th[:], bank_b(q, g)[:].rearrange(order, j=2, u=2, e=2), ACT.Tanh)
                nc.vector.tensor_tensor(
                    hb[q // 2, g][:, :, :, q % 2, :, :],
                    bank_a(q, g)[:].rearrange(order, j=2, u=2, e=2),
                    th[:],
                    ALU.mult,
                )

        def turn(b):
            for g in range(2):
                words = hb[b, g][:].rearrange("n u j c m e -> n (u j c m e)").bitcast(F32)
                for j in range(2):
                    for u in range(2):
                        nc.tensor.transpose(
                            bank_turn(b, g)[:, P * (2 * j + u) : P * (2 * j + u + 1)],
                            words[:, P * (2 * u + j) : P * (2 * u + j + 1)],
                            ident[:],
                        )
                nc.scalar.copy(
                    out=hq[b, g][:].bitcast(F32).rearrange("p (j n) u -> p j n u", j=2),
                    in_=bank_turn(b, g)[:].rearrange("p (j u n) -> p j n u", j=2, u=2),
                )
                nc.vector.quantize_mx(
                    out=hc[b][:, 2 * P * g : 2 * P * (g + 1)].bitcast(FP8X4),
                    scales=hs[b][:, 2 * P * g : 2 * P * (g + 1)],
                    in_=hq[b, g][:].rearrange("p n t -> p (n t)"),
                )

        for a in range(K_PASSES):
            nc.vector.tensor_copy(vs[a][:], tabs[:, a, :].indirect(offs_sb[:]))
        for a in range(K_PASSES):
            gather_queries(a, 2 if a == LAST_PASS else 1)
            round_w1(0, a, SCALAR_COLUMNS_FIRST[a])
            quantise_w1(0, a)
            multiply_b(0, a)
            multiply_a(0, a)
        nc.vector.tensor_copy(v2s[:], tab2s[:].indirect(offs2_sb[:]))
        for q in range(1, QUARTERS):
            if q < LAST_QUARTER:
                gate(q - 1)
            for a in range(K_PASSES):
                round_w1(q, a, SCALAR_COLUMNS_LATER[a])
                quantise_w1(q, a)
                multiply_b(q, a)
            for a in range(K_PASSES):
                multiply_a(q, a)
        gate(LAST_QUARTER - 1)
        gate(LAST_QUARTER)
        for b in range(R_PASSES):
            turn(b)
        nc.scalar.activation(warm[:, 0:2], bank_turn(1, 1)[:, 0:2], ACT.Abs_reciprocal_sqrt, bias=1.0, scale=0.0)

        first = keep.tile([P, R_PASSES, 2 * P], U32, name="first", tag="th_last", align_bytes=64)
        late = keep.tile([P, LIGAND_TILES // 2 - 1, R_PASSES, 2 * P], U32, name="late", tag="hq11", align_bytes=64)

        def ligand_words(b, pair):
            return first[:, b, :] if pair == 0 else late[:, pair - 1, b, :]

        for pair in range(LIGAND_TILES // 2):
            for b in range(R_PASSES):
                nc.vector.tensor_copy(
                    ligand_words(b, pair), tab2w[b][:].bitcast(U32).indirect(offs2_sb[:, 16 * pair : 16 * (pair + 1)])
                )
        for i in range(LIGAND_TILES):
            pair = i // 2
            bank = banks[Y_BANKS[i]]
            for b in range(R_PASSES):
                nc.tensor.matmul_mx(
                    out=bank[:],
                    lhsT=ligand_words(b, pair)[:, P * (i % 2) : P * (i % 2 + 1)].bitcast(FP8X4),
                    lhsT_scale=v2s[LIGAND_PLANE + 4 * b : P, P * i : P * (i + 1)],
                    rhs=hc[b][:].bitcast(FP8X4),
                    rhs_scale=hs[b][:],
                    start=(b == 0),
                    stop=(b == R_PASSES - 1),
                )

        sq = [
            keep.tile([P, S], F32, name="sq%d" % i, tag="w1raw%d%d" % (i // K_PASSES, i % K_PASSES), align_bytes=64)
            for i in range(LIGAND_TILES)
        ]
        dist = {i: keep.tile([P, S], F32, name="dist%d" % i, align_bytes=64) for i in SQUARE_ON_VECTOR}
        for i in SQUARE_ON_VECTOR:
            nc.vector.tensor_scalar(dist[i][:], banks[Y_BANKS[i]][:], -1.0, None, ALU.add)
        for i in SQUARE_ON_VECTOR:
            nc.vector.scalar_tensor_tensor(sq[i][:], banks[Y_BANKS[i]][:], -1.0, dist[i][:], ALU.add, ALU.mult)
        on_scalar = [i for i in range(LIGAND_TILES) if i not in SQUARE_ON_VECTOR]
        for i in range(LIGAND_TILES):
            if i < len(on_scalar):
                j = on_scalar[i]
                nc.scalar.activation(sq[j][:], banks[Y_BANKS[j]][:], ACT.Square, bias=1.0, scale=-1.0)
            rs = ring.tile([P, S], F32, name="rs", bufs=6)
            res = ring.tile([P, S], F32, name="res", bufs=LIGAND_TILES)
            pieces = 2 if i == LIGAND_TILES - 1 else 1
            n = S // pieces
            for s in range(pieces):
                part = slice(n * s, n * (s + 1))
                nc.scalar.activation(rs[:, part], sq[i][:, part], ACT.Abs_reciprocal_sqrt, bias=1.0)
                engine = nc.gpsimd if i in LAST_SQUARE_ON_GPSIMD else nc.vector
                engine.tensor_tensor(res[:, part], rs[:, part], rs[:, part], ALU.mult)
                nc.sync.dma_start(out=out[P * i : P * (i + 1), part], in_=res[:, part])
